import numpy as np, ml_dtypes
CORES = [1,5,17,21,33,37,49,53]
N = 8
BF = ml_dtypes.bfloat16
V, M, S, CAP, P, RO, STEP, LN = 2048, 4096, 256, 40, 12, 2, 950, 3
W1 = 13 * np.arange(16) + 5; W2 = 255 - 14 * np.arange(16); A = N * CAP
def mix(d):
    u = np.add.reduce(W1[:, None] * d, axis=2) & 4095; w = np.add.reduce(W2[:, None] * d, axis=2) & 4095
    return u, (u * w) >> 5
def kid(d, c, hm, t):
    R, n = d.shape[0], d.shape[3]
    hv = np.take_along_axis(hm, d.reshape(R, 8, 1, 16 * n), 3).reshape(R, 8, 16, 16, n)
    e = np.add.reduce(np.minimum(hv, np.abs(c)[:, :, :, None]), axis=2)
    k = np.argmax(e, axis=2); u, h = mix(d); v = (h + 37 * np.max(e, axis=2) + t) & 4095
    void = np.any(d == v[:, :, None], axis=2) | (v >= M)
    new = np.where(np.arange(16)[:, None] == k[:, :, None], v[:, :, None], d)
    q = np.add.reduce((new < v[:, :, None]).astype(np.int64), axis=2)
    return ~void, np.sort(new, axis=2), np.where((((q - k) & 1) == 1)[:, :, None], -(c >> 2), c >> 2)
def spawn(D, C, hm, t):
    start = STEP * (t + 1); a = np.roll(np.any(C != 0, axis=2), -start, axis=2)
    o = np.argsort(~a, axis=2, kind="stable")[:, :, :S]; on = np.take_along_axis(a, o, 2); pl = (o + start) & (V - 1)
    good, ch, c = kid(np.take_along_axis(D, pl[:, :, None], 3), np.take_along_axis(C, pl[:, :, None], 3), hm, t)
    return pl, on, on & good, ch, c
def recs(rng, shape):
    return np.sort(rng.integers(0, M - 15, shape), axis=-2) + np.arange(16)[:, None]
def base(rng, share=None):
    lim = rng.choice(np.array([1, 3, 20, 127]), (N, 8, 1, V), p=[0.15, 0.15, 0.2, 0.5]); C = rng.integers(-lim, lim + 1, (N, 8, 16, V))
    if share is None: share = rng.choice(np.array([0.4, 0.55, 0.75, 0.92]), (N, 8, 1, 1))
    C = C * (rng.random((N, 8, 1, V)) < share)
    return recs(rng, (N, 8, 16, V)), C, rng.integers(0, 128, (N, 8, 16, M))
def plant(rng, D, C, hm, part, twin=False, t=0, own=False):
    live = np.any(C != 0, axis=2); pl, on, good, ch, c = spawn(D, C, hm, t); u, h = mix(ch)
    busy = np.zeros((N, 8, V), bool); np.put_along_axis(busy, pl, on, 2)
    q, g, s = np.nonzero(good & (rng.random(good.shape) < part)); r = h[q, g, s] & (N - 1)
    p = ((h[q, g, s] >> LN) + rng.integers(0, P, q.size) * (2 * u[q, g, s] + 1)) & (V - 1)
    one = np.unique((r * 8 + g) * V + p, return_index=True)[1]
    if not own: one = one[~busy[r[one], g[one], p[one]]]
    q, g, s, r, p = q[one], g[one], s[one], r[one], p[one]
    rec = ch[q, g, :, s]; w = c[q, g, :, s]; lv = live[r, g, p][:, None]; bs = busy[r, g, p][:, None]; n = one.size
    if twin:
        nxt = np.concatenate([rec[:, 1:], np.full((n, 1), M)], axis=1); way = rng.random(n)
        fit = (rec[:, :14] + 1 < rec[:, 1:15] - 2) & (rec[:, 2:] + 1 < nxt[:, 2:]); i = np.argmax(fit * (0.01 + rng.random(fit.shape)), axis=1)
        z = np.nonzero(np.any(fit, axis=1) & (way < 0.4))[0]
        rec[z, i[z]] += 1; rec[z, i[z] + 1] -= 2; rec[z, i[z] + 2] += 1
        i = np.where(rng.random(n) < 0.3, 15, rng.integers(0, 16, n))
        z = np.nonzero((way > 0.6) & (rec[np.arange(n), i] + 1 < nxt[np.arange(n), i]))[0]
        rec[z, i[z]] += 1
    D[r, g, :, p] = rec
    mode = rng.integers(0, 4, (n, 1)); old = C[r, g, :, p]; some = np.any(w != 0, axis=1)[:, None]
    new = np.where(lv & (mode == 0) & some, -w, np.where(lv & (mode == 1), np.where(w < 0, -127, 127), old))
    C[r, g, :, p] = np.where(bs & (mode == 3), rng.choice(np.array([-1, 1]), (n, 16)), new)
def pack(D, C, hm):
    return {"det": np.ascontiguousarray((256 * D + C + 128).reshape(N, 128, V)).astype(np.int32), "ham": np.ascontiguousarray(hm.reshape(N, 128, M)).astype(np.float32).astype(BF)}
def setup_inputs(rng):
    D, C, hm = base(rng)
    for t in range(RO - 1, -1, -1): plant(rng, D, C, hm, 0.35, False, t, True)
    return pack(D, C, hm)
def setup_inputs_slots(rng):
    D, C, hm = base(rng, 2.0); C[:, :, 0] = np.where(np.any(C != 0, axis=2), C[:, :, 0], 1)
    for q in range(N):
        good, ch, c = kid(D[q:q + 1], C[q:q + 1], hm[q:q + 1], 0); mine = good[0] & ((mix(ch)[1][0] & (N - 1)) == ((q + 1) & (N - 1)))
        for g in range(8):
            hit = rng.permutation(np.nonzero(mine[g])[0]); rest = rng.permutation(np.nonzero(~mine[g])[0])
            n = min((CAP, CAP + 1, CAP - 1, S, 0, 1, CAP, CAP + 1)[g], len(hit))
            seq = np.concatenate([rng.permutation(np.concatenate([hit[:n], rest[:S - n]])), rng.permutation(np.concatenate([hit[n:], rest[S - n:]]))])
            k = int(rng.integers(S, V - 63)); o = rng.permutation(V); at = (np.concatenate([np.sort(o[:k]), o[k:]]) + STEP) & (V - 1)
            d2 = np.zeros_like(D[q, g]); c2 = np.zeros_like(C[q, g])
            d2[:, at] = D[q, g][:, seq]; c2[:, at[:k]] = C[q, g][:, seq[:k]]; D[q, g] = d2; C[q, g] = c2
    return pack(D, C, hm)
def setup_inputs_ties(rng):
    D, C, hm = base(rng); ev = np.ascontiguousarray(D[:, ::2]); u, h = mix(ev)
    x = np.take_along_axis(ev, rng.integers(0, 16, (N, 4, 1, V)), 2); y = np.take_along_axis(ev, rng.integers(0, 16, (N, 4, 1, V)), 2)
    goal = rng.permuted(np.concatenate([x, x + 1, x - 1, y, y + 1, ev[:, :, :1], ev[:, :, 15:], 0 * x, 0 * x + M - 1, 0 * x + 4095], axis=2), axis=2)
    e = ((goal - h[:, :, None]) * pow(37, -1, 4096)) & 4095; ok = (e >= 1) & (e <= 2032)
    e = np.take_along_axis(e, np.argmax(ok, axis=2)[:, :, None], 2); ok = np.any(ok, axis=2)[:, :, None]
    z = (np.arange(16)[:, None] + rng.integers(0, 16, (N, 4, 1, V))) & 15
    new = ((e >> 4) + (z < (e & 15))) * rng.choice(np.array([-1, 1]), (N, 4, 16, V)); live = np.any(C[:, ::2] != 0, axis=2)[:, :, None]
    C[:, ::2] = np.where(ok & live, new, C[:, ::2])
    hm[:, ::2] = 127; hm[:, 1::2] = rng.choice(np.array([0, 9, 60]), (N, 4, 1, M))
    hm[np.arange(N), 2 * rng.integers(0, 4, N) + 1] = 0
    plant(rng, D, C, hm, 0.2)
    return pack(D, C, hm)
def setup_inputs_twins(rng):
    D, C, hm = base(rng); hm = np.repeat(hm[:1], N, axis=0); ix = rng.integers(0, 40, (N, 8, 1, V))
    pd = np.repeat(recs(rng, (1, 8, 16, 40)), N, axis=0)
    pc = np.repeat(np.where(np.arange(40) < 12, rng.integers(0, 4, (1, 8, 16, 40)), rng.integers(4, 128, (1, 8, 16, 40))), N, axis=0)
    use = rng.random((N, 8, 1, V)) < 0.6; live = np.any(C != 0, axis=2)[:, :, None]
    sign = np.where(rng.random((N, 8, 1, V)) < 0.4, 1, rng.choice(np.array([-1, 1]), (N, 8, 16, V)))
    D = np.where(use, np.take_along_axis(pd, ix, 3), D)
    C = np.where(use & live, np.take_along_axis(pc, ix, 3) * sign, C)
    plant(rng, D, C, hm, 0.5); plant(rng, D, C, hm, 0.4); plant(rng, D, C, hm, 0.4, True)
    return pack(D, C, hm)
def setup_inputs_thin(rng):
    D, C, hm = base(rng, 2.0); lone = np.arange(16)[:, None] == rng.integers(0, 16, (N, 8, 1, V))
    C[:, 1::2] = np.where(lone, np.where(C == 0, -1, C), 0)[:, 1::2]
    C[:, :, 0] = np.where(np.any(C != 0, axis=2), C[:, :, 0], 1); sizes = np.array([0, 1, 5, S - 1, S, S + 1, V - 1, V])
    for q in range(N):
        for g in range(8):
            n = int(sizes[g]) if q == 0 else int(rng.choice(sizes)); o = rng.permutation(V)
            if n == 5: o = np.array([0, V - 1, STEP - 1, STEP, STEP + 1])
            keep = np.zeros(V, np.int64); keep[o[:n]] = 1; C[q, g] = C[q, g] * keep
    plant(rng, D, C, hm, 0.3)
    return pack(D, C, hm)
def setup_inputs_spread(rng):
    D, C, hm = base(rng)
    D = np.sort(((M - 15) * rng.random((N, 8, 16, V)) ** rng.choice(np.array([1.0, 4.0]), (N, 8, 1, V))).astype(np.int64), axis=2) + np.arange(16)[:, None]
    size = np.exp2(7 * rng.random((N, 8, 1, V))); live = np.any(C != 0, axis=2)[:, :, None]
    C = np.minimum((size * rng.random((N, 8, 16, V))).astype(np.int64), 127) * rng.choice(np.array([-1, 1]), (N, 8, 16, V)) * live
    hm = np.minimum((np.exp2(7 * rng.random((N, 8, 1, M))) * rng.random((N, 8, 16, M))).astype(np.int64), 127)
    plant(rng, D, C, hm, 0.3)
    return pack(D, C, hm)
def check_inputs(d):
    bad = []
    x = d["det"].astype(np.int64).reshape(N, 8, 16, V); o = x >> 8
    if np.min(o) < 0 or np.max(o) > M - 1: bad.append("orbitals of det")
    if np.min(x & 255) < 1: bad.append("counts of det")
    if not np.all(o[:, :, 1:] > o[:, :, :-1]): bad.append("rising orbitals of det")
    h = d["ham"].astype(np.float32)
    if not np.all((h >= 0) & (h <= 127) & (h == np.floor(h))): bad.append("numbers of ham")
    return bad
def reference(det, ham):
    x = det.astype(np.int64).reshape(N, 8, 16, V); D = x >> 8; C = (x & 255) - 128
    hm = ham.astype(np.float32).astype(np.int64).reshape(N, 8, 16, M); num = np.arange(P)[:, None]
    for t in range(RO):
        pl, on, good, ch, c = spawn(D, C, hm, t)
        sel = np.zeros((N, 8, V), bool); np.put_along_axis(sel, pl, on, 2)
        C = C - np.sign(C) * sel[:, :, None]
        f = good[:, :, None] & ((mix(ch)[1] & (N - 1))[:, :, None] == np.arange(N)[:, None])
        before = np.add.accumulate(f.astype(np.int64), axis=3) - f.astype(np.int64)
        q, g, r, s = np.nonzero(f & (before < CAP)); a = q * CAP + before[q, g, r, s]
        ad = np.zeros((N, 8, 16, A), np.int64); ac = np.zeros((N, 8, 16, A), np.int64); there = np.zeros((N, 8, A), bool)
        ad[r, g, :, a] = ch[q, g, :, s]; ac[r, g, :, a] = c[q, g, :, s]; there[r, g, a] = True
        u, h = mix(ad)
        p = ((h >> LN)[:, :, None] + num * (2 * u + 1)[:, :, None]) & (V - 1)
        live = np.any(C != 0, axis=2); lp = np.take_along_axis(live, p.reshape(N, 8, P * A), 2).reshape(N, 8, P, A)
        dp = np.take_along_axis(D, p.reshape(N, 8, 1, P * A), 3).reshape(N, 8, 16, P, A)
        same = np.all(dp == ad[:, :, :, None], axis=2) & lp
        score = np.where(same, num, np.where(lp, 2 * P, P + num))
        ok = there & (np.min(score, axis=2) < 2 * P); place = np.take_along_axis(p, np.argmin(score, axis=2)[:, :, None], 2)[:, :, 0]
        r, g, a = np.nonzero(ok); low = np.full((N, 8, V), A); np.minimum.at(low, (r, g, place[r, g, a]), a)
        r, g, a = np.nonzero(ok & (np.take_along_axis(low, place, 2) == np.arange(A))); b = place[r, g, a]
        D[r, g, :, b] = ad[r, g, :, a]; C[r, g, :, b] = np.clip(C[r, g, :, b] + ac[r, g, :, a], -127, 127)
    return {"y": (256 * D + C + 128).reshape(N, 128, V).astype(np.float32)}

@@ -1,0 +1,639 @@
+from concourse.bass import DstId, RemoteDMATransfer
+from concourse.mybir import AluOpType as A, AxisListType, ActivationFunctionType as F
+
+N, V, CAP, S, RO, STEP, NP = 8, 2048, 40, 256, 2, 950, 12
+AR = N * CAP
+TR = 320
+M31 = 1.5 * 2.0 ** 31
+M27 = 1.5 * 2.0 ** 27
+M23 = 1.5 * 2.0 ** 23
+OFF = 2.0 ** 22
+SENT = -22528
+THETA = 1.14e10
+
+_DT = {"f": "float32", "b": "bfloat16", "h": "float16", "i": "int32", "u": "uint16"}
+_SBUF = """
+f X:2368 Y:2368 J:256 JI:128 JG:128 PD:128 jm6:144 jm15:144 jm11:144 tm:144 tm2:144 col:32 ones:128 sw:20 swj:16 swp:16 swh:16 Jp:256
+f dtr:20 c9f:144 m16:256 MX:16 E:128 U:136 acs:16 acv:16 cb:16 vw:16 dm8:16 fo:16 fo2:16 fo3:16 T6:256 Sx:256 C:256 Ks:256 hb:16
+f rk:16 VK:512 R1:256 R2:256 m1:256 FK:256 cc:256 PK:256 iv:16 iv2:16 own:16 I9:144 A9:144 s9:144 t64:64 t32:32 t16:16 slf:16
+f SL0:2304 SL1:2304 LA0:320 LA1:320 Cf:256 xf:256 xg:256 Q1:320 ac:320 st:24 s2:32 s4:64 s8:64 dd:3840 KS:60 K1:60 K2:60 K3:32
+f km:20 ms:20 va:20 pv:20 dp:20 dp2:20 lw:20 l2:20 wn:20 eo:20 eo2:20 w1:320 xm:320 xk:320 cn:320 ck:320 cq:320 xn:320 xo:320
+f R4:4,32 R5:5,32
+i XI:2048 X1:2048 pp_i:1 pq_i:1 ai:16 pl:16 hp:16 hq:16 vi:16 vv:16 Fl:256 ch:16 ow:16 ah:16 Hh:20 Z:192 Zm:192 mi:20 ma:20 pz:20 pm:20
+i hi:2,16 ha:2,16 ci:4,8 ca:4,8 ai5:5,8 aa5:5,8
+h NZ:2048 BH:128 NU:128 SU:128 SD:128 ID:128 BI:128 PAR:128 PK1:128 PK2:128 WT:16 EH:144 OH:144 E1:144 O1:144 e0h:128 RX:2048 CM:320
+h c9:144 Lb:128 G:256 Dh:256 VB:512 mA:256 mB:256 ow1:256 O:144 pvh:20 Pr:320
+h CH:16,16 eq:16,16 A16:20,16
+b HM:4096 SG:2064 BB:128 AL:128 ZS:144 I592:8 e0b:128 kc:128 kcm:240 ID32:128 ID8:128 m16b:320 cmp:1024 jnk:2048 Lg:4096 Mn:4096
+b fsq:256 fsg:256 sq:3840 k1:240 k2:240 EQ:3040 DG:320 DS:320 esq:320 esg:320
+u cu:16 plu:16 fou:16 Du:256 slu:16 zu:256 pu:20 eou:20
+"""
+_ALL, SCRATCH, _AT = {}, {}, {}
+for _line in _SBUF.split("\n"):
+    _w = _line.split()
+    for _e in _w[1:]:
+        _n, _s = _e.split(":")
+        _ALL[_n] = ("sbuf", [128] + [int(_k) for _k in _s.split(",")], _DT[_w[0]])
+for _n in ("P0", "P1", "P2", "P3", "P4", "P5"):
+    _ALL[_n] = ("psum", [128, 512], "float32")
+for _n in ("Q0", "Q1p"):
+    _ALL[_n] = ("psum", [128, 16, 32], "float32")
+_wide = {}
+for _n, (_w, _sh, _d) in _ALL.items():
+    if _w == "sbuf" and len(_sh) == 2 and _sh[1] <= 144:
+        _AT[_n] = ("pack_" + _d, _wide.get(_d, 0))
+        _wide[_d] = _AT[_n][1] + -(-_sh[1] // 16) * 16
+    else:
+        SCRATCH[_n] = (_w, _sh, _d)
+for _d, _c in _wide.items():
+    SCRATCH["pack_" + _d] = ("sbuf", [128, _c], _d)
+SEMAPHORES = ["sv", "ss", "sp", "sg", "loc", "ar0", "ar1", "an0", "an1"] + ["d%d" % k for k in range(7)]
+_PSUM = ("P0", "P1", "P2", "P3", "P4", "P5", "Q0", "Q1p")
+
+
+def routes(src, T, topo):
+    r = T.rank_of(src)
+    ring = [T.cores[(r + k) % N] for k in range(1, N)]
+    near = [d for d in ring if topo.chip(d) == topo.chip(src)]
+    far = [d for d in ring if topo.chip(d) != topo.chip(src)]
+    eng = topo.engines(src, far[0])
+    n = len(eng)
+    out = [(0, d, eng[k * n // 4:(k + 1) * n // 4]) for k, d in enumerate(far[:4])]
+    out += [(1, d, eng[k * n // 2:(k + 1) * n // 2]) for k, d in enumerate(far[4:])]
+    return out + [(0, d, [e for e in topo.engines(src, d) if e not in eng]) for d in near]
+
+
+def landing(dst, T, topo):
+    near = [c for c in T.cores if topo.chip(c) == topo.chip(dst)]
+    return [T.rank_of(c) for c in near + [c for c in T.cores if c not in near]]
+
+
+def rank_program(g, core, T, topo):
+    me = T.rank_of(core)
+    if me is None:
+        return
+    queue = {"v": g.vector, "s": g.scalar, "p": g.tensor, "g": g, "y": g.sync}
+    semof = {"v": "sv", "s": "ss", "p": "sp", "g": "sg"}
+    cnt, known, snap, acc = {}, {e: {} for e in queue}, {}, {}
+    BIGC = 1000000
+
+    def b(n, lo=0, hi=None, step=1):
+        if hi is None:
+            hi = _ALL[n][1][1]
+        if n in _AT:
+            w, at = _AT[n]
+            return T[w][:, at + lo:at + hi:step], [(w, at + lo, at + hi)]
+        return T[n][:, lo:hi:step], [(n, lo, hi)]
+
+    full = slice(None)
+
+    def b3(n, s1=full, s2=full):
+        return T[n][:, s1, s2], [(n, 0, BIGC)]
+
+    def ind(w, o):
+        return w[0].indirect(o[0]), w[1] + o[1]
+
+    def need(e, reads, writes):
+        want = {}
+        for kind, keys in ((0, reads), (1, writes)):
+            for (n, lo, hi) in keys:
+                ps = n in _PSUM
+                for lo2, hi2, k2, sem, val, e2 in acc.get(n, []):
+                    if not ps and not (lo < hi2 and lo2 < hi):
+                        continue
+                    if e == "p" and e2 == "p" or not (kind or k2 or ps and e != e2):
+                        continue
+                    want[sem] = max(want.get(sem, 0), val)
+        kn = known[e]
+        for s, v in sorted(want.items(), key=lambda x: (x[0] == semof.get(e), x[0])):
+            if kn.get(s, 0) >= v:
+                continue
+            queue[e].wait_ge(T.sem[s], v)
+            kn[s] = v
+            for s2, v2 in snap.get((s, v), {}).items():
+                kn[s2] = max(kn.get(s2, 0), v2)
+
+    def note(e, reads, writes, sem, val):
+        for kind, keys in ((0, reads), (1, writes)):
+            for (n, lo, hi) in keys:
+                if n in _PSUM:
+                    lo, hi = 0, BIGC
+                lst = acc.setdefault(n, [])
+                lst[:] = [r for r in lst if not (kind and lo <= r[0] and r[1] <= hi)
+                          and not (r[5] == e and r[2] == kind and r[3] == sem and r[0] == lo and r[1] == hi)]
+                lst.append((lo, hi, kind, sem, val, e))
+
+    def op(e, call, outs, ins):
+        reads = [k for x in ins for k in x[1]]
+        writes = [k for x in outs for k in x[1]]
+        need(e, reads, writes)
+        s = semof[e]
+        cnt[s] = v = cnt.get(s, 0) + 1
+        call().then_inc(T.sem[s], 1)
+        snap[(s, v)] = dict(known[e])
+        note(e, reads, writes, s, v)
+
+    def dma(e, out, in_, sem):
+        need(e, in_[1], out[1])
+        queue[e].dma_start(out=out[0], in_=in_[0]).then_inc(T.sem[sem], 16)
+        snap[(sem, 16)] = dict(known[e])
+        note(e, in_[1], out[1], sem, 16)
+
+    def sc(x):
+        return x[0] if isinstance(x, tuple) else x
+
+    def ts(out, in0, s1, s2, op0, op1=None):
+        ins = [in0] + [x for x in (s1, s2) if isinstance(x, tuple)]
+        if op1 is None:
+            op("v", lambda: g.vector.tensor_scalar(out[0], in0[0], sc(s1), None, op0), [out], ins)
+        else:
+            op("v", lambda: g.vector.tensor_scalar(out[0], in0[0], sc(s1), sc(s2), op0, op1), [out], ins)
+
+    def tt(out, in0, in1, o):
+        op("v", lambda: g.vector.tensor_tensor(out[0], in0[0], in1[0], o), [out], [in0, in1])
+
+    def cp(out, in_):
+        op("v", lambda: g.vector.tensor_copy(out[0], in_[0]), [out], [in_])
+
+    def scan(out, d0, d1, o0, o1):
+        op("v", lambda: g.vector.tensor_tensor_scan(out[0], d0[0], d1[0], 0.0, o0, o1), [out], [d0, d1])
+
+    def red(out, in_, o):
+        op("v", lambda: g.vector.tensor_reduce(out[0], in_[0], AxisListType.X, o), [out], [in_])
+
+    def vtr(out, in_):
+        op("v", lambda: g.vector.transpose(out[0], in_[0]), [out], [in_])
+
+    def act(out, in_, f, bias=0.0, scale=1.0, accum=None):
+        ins = [in_] + [x for x in (bias, scale) if isinstance(x, tuple)]
+        if accum is None:
+            op("s", lambda: g.scalar.activation(out[0], in_[0], f, bias=sc(bias), scale=sc(scale)), [out], ins)
+        else:
+            op("s", lambda: g.scalar.activation(out[0], in_[0], f, bias=sc(bias), scale=sc(scale), accum_out=accum[0]), [out, accum], ins)
+
+    def mm(out, l, r, start=True, stop=True):
+        op("p", lambda: g.tensor.matmul(out[0], l[0], r[0], start, stop), [out], [l, r])
+
+    def iota(n, pat, base, cm, lo=0, hi=None):
+        out = b(n, lo, hi)
+        if _ALL[n][2] == "int32":
+            op("g", lambda: g.iota(out[0], pat, base, cm), [out], [])
+        else:
+            op("g", lambda: g.iota(out[0], pat, base, cm, allow_small_or_imprecise_dtypes=True), [out], [])
+
+    for k in range(4):
+        dma("y", b("XI", 512 * k, 512 * k + 512), (T.det[:, 512 * k:512 * k + 512], []), "d%d" % k)
+    dma("s", b("HM"), (T.ham[:], []), "d4")
+
+    iota("pp_i", [[0, 1]], 0, 1)
+    iota("JG", [[1, 8], [0, 16]], 0, 0)
+    iota("jm15", [[1, 144]], -15, 0)
+    iota("JI", [[0, 8], [1, 16]], 0, 0)
+    iota("PD", [[1, 128]], 0, -1)
+    iota("swj", [[16, 4], [64, 4]], 0, 0)
+    iota("J", [[1, 256]], 0, 0)
+    iota("jm11", [[1, 144]], -11, 0)
+    iota("ones", [[0, 128]], 1, 0)
+    iota("U", [[0, 8]], -1, 0, 128, 136)
+    iota("Jp", [[16, 4], [64, 4], [1, 16]], 0, 0)
+    iota("jm6", [[1, 144]], -6, 0)
+    iota("c9f", [[256, 9], [0, 16]], -1, 0)
+    iota("VK", [[0, 512]], 0, 0)
+    for o in range(N):
+        iota("SL0", [[0, CAP]], SENT, 0, 256 * o, 256 * o + CAP)
+    iota("kcm", [[-1, 12], [0, 5]], 8, 0, 0, 60)
+    iota("kcm", [[-1, 12], [0, 15]], 8, 0, 60, 240)
+    iota("lw", [[0, 20]], 0, 0)
+    iota("st", [[0, 24]], 0, 0)
+    iota("Z", [[0, 192]], 0, 0)
+    for o in range(N):
+        iota("SL1", [[0, CAP]], SENT, 0, 256 * o, 256 * o + CAP)
+
+    PI, PG16, PGE, PGO, IM, ACOL, BCOL, W1, W2, SIG, WAL, P0C, PGE1, PGO1, SIGK, SIGM, E0C, N15, OD, PP, N0 = \
+        [b("col", k, k + 1) for k in range(21)]
+    q_i = b("pq_i")
+    ts(q_i, b("pp_i"), 15, None, A.bitwise_and)
+    ts(PI, q_i, 1.0, None, A.mult)
+    ts(q_i, b("pp_i"), 4, None, A.arith_shift_right)
+    ts(PG16, q_i, 16.0, None, A.mult)
+    ts(OD, q_i, 1.0, None, A.mult)
+    ts(b("BH"), b("JG"), OD, None, A.is_equal)
+    ts(b("ZS"), b("jm15"), PG16, None, A.is_equal)
+    ts(E0C, PI, 0.0, OFF, A.is_equal, A.mult)
+    ts(WAL, PI, 1.0, -128.0, A.is_equal, A.mult)
+    tt(WAL, WAL, E0C, A.add)
+    ts(b("AL"), b("BH"), WAL, None, A.mult)
+    ts(b("tm", 0, 128), b("PD"), 0.0, -1.0, A.is_lt, A.mult)
+    tt(b("NU"), b("tm", 0, 128), b("BH"), A.mult)
+    ts(q_i, q_i, 1, None, A.bitwise_and)
+    cp(OD, q_i)
+    ts(PGE, OD, 100000.0, PG16, A.mult, A.add)
+    ts(PGO, OD, -100000.0, 100000.0 - 16.0, A.mult, A.add)
+    tt(PGO, PGO, PG16, A.add)
+    ts(b("E1"), b("jm11"), PGE, None, A.is_equal)
+    ts(b("O1"), b("jm11"), PGO, None, A.is_equal)
+    ts(b("sw"), b("J", 0, 20), 16.0, PI, A.mult, A.add)
+    ts(b("swp"), b("swj"), PI, None, A.add)
+    ts(b("swh"), b("swp"), 0.5, None, A.add)
+
+    def spawn_constants():
+        ts(b("ID"), b("PD"), 0.0, None, A.is_equal)
+        ts(W1, PI, 13.0, 5.0, A.mult, A.add)
+        ts(W2, PI, -14.0, 255.0, A.mult, A.add)
+        ts(P0C, b("pp_i"), 0.0, None, A.is_equal)
+        ts(b("WT", 0, 8), b("BH", 0, 128, 16), W1, None, A.mult)
+        ts(b("WT", 8, 16), b("BH", 0, 128, 16), W2, None, A.mult)
+        ts(b("e0b"), b("J", 0, 128), 0.0, P0C, A.mult, A.add)
+        ts(b("kc"), b("JI"), -1.0, 7.5, A.mult, A.add)
+        ts(b("I592"), b("BH", 0, 128, 16), 592.0, None, A.mult)
+        ts(b("m16", 0, 128), b("JI"), 0.0, None, A.is_gt)
+        cp(b("m16", 128, 256), b("m16", 0, 128))
+        ts(IM, PI, -7.5, None, A.add)
+        ts(N0, PI, 0.0, None, A.is_gt)
+        ts(N15, PI, 15.0, None, A.is_lt)
+        ts(ACOL, N15, -1.0, None, A.mult)
+        ts(BCOL, N0, -1.0, None, A.add)
+        ts(b("SU"), b("PD"), -1.0, N0, A.is_equal, A.mult)
+        ts(b("SD"), b("PD"), 1.0, N15, A.is_equal, A.mult)
+        ts(b("BI"), b("PD"), 0.0, 8192.0, A.is_equal, A.mult)
+        ts(q_i, b("pp_i"), 1, None, A.bitwise_and)
+        ts(SIG, q_i, -2.0, 1.0, A.mult, A.add)
+        ts(SIGK, SIG, 1.0 / 256.0, None, A.mult)
+        ts(SIGM, SIG, -1.0 / 256.0, None, A.mult)
+        ts(b("PAR"), b("BH"), SIG, None, A.mult)
+        ts(b("PK1"), b("BH"), SIGK, None, A.mult)
+        ts(b("PK2"), b("BH"), SIGM, None, A.mult)
+        ts(PGE1, PGE, 1.0, None, A.add)
+        ts(PGO1, PGO, 1.0, None, A.add)
+        for n, c0, c1 in (("EH", PGE, PGE1), ("OH", PGO, PGO1)):
+            ts(b("tm2"), b("jm6"), c0, W1, A.is_equal, A.mult)
+            ts(b("tm"), b("jm6"), c1, W2, A.is_equal, A.mult)
+            tt(b(n), b("tm"), b("tm2"), A.add)
+        cp(b("e0h"), b("e0b"))
+        cp(b("c9"), b("c9f"))
+
+    def arrival_constants():
+        cp(b("BB"), b("BH"))
+        ts(b("ID32"), b("ID"), 32.0, None, A.mult)
+        ts(b("ID8"), b("ID"), 8.0, None, A.mult)
+        ts(b("MX"), b("J", 0, 16), PI, None, A.is_equal)
+        for x in range(16):
+            ts(b("RX", 128 * x, 128 * x + 128), b("BH"), b("MX", x, x + 1), None, A.mult)
+        for lo, hi in ((0, 128), (128, 256), (256, 320)):
+            ts(b("CM", lo, hi), b("JI", 0, hi - lo), PI, 0.5, A.is_ge, A.mult)
+            cp(b("m16b", lo, hi), b("m16", 0, hi - lo))
+        ts(b("dtr"), b("sw"), -1.0, float(TR), A.mult, A.add)
+
+    def q4(k):
+        return 512 * k, 512 * k + 512
+    for k in range(4):
+        ts(b("X1", *q4(k)), b("XI", *q4(k)), 255, None, A.bitwise_and)
+        ts(b("NZ", *q4(k)), b("X1", *q4(k)), 128.0, None, A.not_equal)
+        mm(b("P%d" % k), b("BH"), b("NZ", *q4(k)))
+        act(b("SG", *q4(k)), b("P%d" % k), F.Sign, bias=-0.5)
+        if k == 0:
+            act(b("SG", V, V + 16), b("P0", 0, 16), F.Sign, bias=-0.5)
+
+    XW = b("X", TR, TR + V)
+    plan = {d: routes(d, T, topo) for d in T.cores}
+    land = {d: landing(d, T, topo) for d in T.cores}
+    near = sum(topo.chip(d) == topo.chip(core) for d in T.cores)
+    own0 = min(land[core][:near])
+    PART = ((0, near * CAP // 16), (near * CAP // 16, AR // 16))
+    sent = [0]
+    EQW, CHW = b3("eq"), b3("CH")
+
+    for t in range(RO):
+        start = STEP * (t + 1)
+        if t:
+            for k in range(4):
+                x = b("X", TR + 512 * k, TR + 512 * k + 512)
+                if k % 2:
+                    ts(b("SG", *q4(k)), x, 0.0, None, A.is_gt)
+                else:
+                    act(b("SG", *q4(k)), x, F.Sign)
+                    if k == 0:
+                        act(b("SG", V, V + 16), b("X", TR, TR + 16), F.Sign)
+        c1 = (V - start + 15) // 16
+        e1 = start + 16 * c1 - V
+        for x in range(16):
+            mm(b("P4", 0, c1), b("ZS", 15 - x, 143 - x), b("SG", start + x, start + x + 16 * (c1 - 1) + 1, 16), x == 0, x == 15)
+        for x in range(16):
+            mm(b("P4", c1, 128), b("ZS", 15 - x, 143 - x), b("SG", e1 + x, e1 + x + 16 * (127 - c1) + 1, 16), x == 0, x == 15)
+        if t == 0:
+            spawn_constants()
+        ts(b("Lb"), b("P4", 0, 128), 0.0, None, A.is_gt)
+        mm(b("P5", 0, 128), b("BH"), b("Lb"))
+        mm(b("P4", 128, 256), b("NU"), b("Lb"))
+        if t == 0:
+            for k in range(4):
+                mm(b("P%d" % k), b("AL"), b("SG", *q4(k)))
+        scan(b("E"), b("ones"), b("P5", 0, 128), A.mult, A.add)
+        NA = 10
+        for k in range(NA):
+            act(b("jnk", 128 * k, 128 * k + 128), b("E"), F.Sign, bias=b("swh", k, k + 1), scale=-1.0, accum=b("acs", k, k + 1))
+        tt(b("U", 0, 128), b("E"), b("P4", 128, 256), A.add)
+        for k in range(NA, 17):
+            if k < 16:
+                ts(b("cmp", 128 * (k - NA), 128 * (k - NA) + 128), b("E"), b("swp", k, k + 1), None, A.is_le)
+            if k > NA:
+                red(b("acv", k - 1, k), b("cmp", 128 * (k - 1 - NA), 128 * (k - NA)), A.add)
+        ts(b("vw"), b("sw", 0, 16), b("E", 127, 128), None, A.is_lt)
+        ts(b("cu", NA, 16), b("acv", NA, 16), 1.0, None, A.mult)
+        ts(b("cu", 0, NA), b("acs", 0, NA), 0.5, 64.0, A.mult, A.add)
+        tt(b("G"), ind(b("U"), b("cu")), b("Jp"), A.is_le)
+        for lo, hi, n, sl, bi in ((0, NA, "acs", 8.0, 1024.0), (NA, 16, "acv", 16.0, 0.0)):
+            for j in range(4):
+                u0, u1 = max(lo, 4 * j), min(hi, 4 * j + 4)
+                if u0 < u1:
+                    ts(b("cb", j + 4 * (u0 - 4 * j), j + 4 * (u1 - 1 - 4 * j) + 1, 4), b(n, u0, u1), sl, bi + start, A.mult, A.add)
+        ts(b("dm8"), b("vw"), -8.0, 8.0, A.mult, A.add)
+        for par, n in ((0, "E1"), (16, "O1")):
+            for j in range(4):
+                mm(b3("Q0", slice(0, 4), slice(par, par + 16)), b(n, 11 - j, 139 - j), b("G", 64 * j, 64 * j + 64), j == 0, j == 3)
+        if t == 0:
+            for k in range(4):
+                tt(b("X", TR + 512 * k, TR + 512 * k + 512), b("XI", *q4(k)), b("P%d" % k), A.add)
+        vtr(b3("R4"), b3("Q0", slice(0, 4), full))
+        tt(b("ai"), b("cb"), b3("R4", full, slice(0, 4)), A.add)
+        ts(b("pl"), b("ai"), V - 1, None, A.bitwise_and)
+        cp(b("plu"), b("pl"))
+        act(b("Sx"), ind(XW, b("plu")), F.Identity, bias=-OFF)
+        ts(b("T6"), ind(XW, b("plu")), M31, -(M31 + OFF), A.add, A.add)
+        ts(b("Du"), b("T6"), 1.0 / 256.0, 4095.0, A.mult, A.min)
+        tt(b("C"), b("Sx"), b("T6"), A.subtract)
+        for lo, hi in ((64, 96), (0, 0), (96, 128), (128, 192), (192, 256)):
+            if lo == hi:
+                act(b("P0", 0, 256), b("C"), F.Abs)
+            else:
+                act(b("Lg", 16 * lo, 16 * hi), ind(b("HM"), b("Du", lo, hi)), F.Copy)
+        ts(b("Dh"), b("T6"), 1.0 / 256.0, -2048.0, A.mult, A.add)
+        cp(b("Lg", 0, 1024), ind(b("HM"), b("Du", 0, 64)))
+        for h in range(2):
+            mm(b("P3", 16 * h, 16 * h + 16), b("Dh", 128 * h, 128 * h + 128), b("WT"))
+        for h in range(2):
+            mm(b("P%d" % (1 + h), 0, 128), b("e0b"), b("kc"), True, False)
+        for qd in range(4):
+            lo, h = 64 * qd, qd // 2
+            for k in range(16):
+                tt(b("Mn", 256 * k + lo, 256 * k + lo + 64), b("Lg", 16 * lo + k, 16 * lo + 1024, 16), b("P0", lo, lo + 64), A.min)
+                if qd % 2:
+                    mm(b("P%d" % (1 + h), k, 128, 16), b("Mn", 256 * k + 128 * h, 256 * k + 128 * h + 128), b("I592"), False, k == 15)
+            if qd == 1:
+                cp(b3("hi"), b("P3", 0, 32))
+                ts(b("Fl"), b("C"), 0.25, -0.375, A.mult, A.add)
+                ts(b3("ha"), b3("hi"), 4095, None, A.bitwise_and)
+                tt(b("hp"), b3("ha", full, slice(0, 8)), b3("ha", full, slice(8, 16)), A.mult)
+                ts(b("hq"), b("hp"), 5, None, A.arith_shift_right)
+                ts(b("hb"), b("hq"), 16.0, M27 + 16.0 * t, A.mult, A.add)
+            if qd == 2:
+                scan(b("Ks", 0, 128), b("m16", 0, 128), b("P1", 0, 128), A.mult, A.max)
+        scan(b("Ks", 128, 256), b("m16", 0, 128), b("P2", 0, 128), A.mult, A.max)
+        kmx = b("Ks", 15, 256, 16)
+        tt(b("vi"), kmx, b("hb"), A.add)
+        ts(b("rk"), kmx, M27, -M27, A.add, A.add)
+        ts(b("vv"), b("vi"), 4, 4095, A.arith_shift_right, A.bitwise_and)
+        tt(b("VK", 256, 512, 16), b("rk"), kmx, A.subtract)
+        ts(b("VK", 0, 256, 16), b("vv"), -2048.0, None, A.add)
+        scan(b("VB", 256, 512), b("m16"), b("VK", 256, 512), A.mult, A.add)
+        scan(b("VB", 0, 256), b("m16"), b("VK", 0, 256), A.mult, A.add)
+        mm(b("P5", 0, 256), b("SU"), b("Dh"), True, False)
+        mm(b("P1", 0, 256), b("SD"), b("Dh"), True, False)
+        for x in (2, 3, 0, 1):
+            mm(b("P4" if x > 1 else "P3", 128 * (x % 2), 128 * (x % 2) + 128), b("VB", 128 * x, 128 * x + 128), b("ID"))
+        kr, vr = b("P4", 0, 256), b("P3", 0, 256)
+        ts(b("mA"), kr, IM, ACOL, A.is_le, A.add)
+        ts(b("mB"), kr, IM, BCOL, A.is_lt, A.add)
+        mm(b("P5", 0, 256), b("BI"), b("mA"), False, True)
+        mm(b("P1", 0, 256), b("BI"), b("mB"), False, True)
+        mm(b("P2", 0, 256), b("PK1"), b("mA"), True, False)
+        mm(b("P2", 0, 256), b("PK2"), b("mB"), False, True)
+        tt(EQW, b("Dh"), vr, A.is_equal)
+        tt(b("R1"), b("Dh"), b("P5", 0, 256), A.max)
+        tt(b("m1"), b("R1"), vr, A.min)
+        tt(b("R2"), b("Dh"), b("P1", 0, 256), A.min)
+        tt(CHW, b("R2"), b("m1"), A.max)
+        for par, ns, nh in ((0, "E1", "EH"), (16, "O1", "OH")):
+            for j in range(4):
+                mm(b3("Q0", slice(0, 4), slice(par, par + 16)), b(ns, 3 - j, 131 - j), b3("eq", slice(j, None, 4), full), j == 0, False)
+            for j in range(4):
+                mm(b3("Q0", slice(0, 4), slice(par, par + 16)), b(nh, 6 - 2 * j, 134 - 2 * j), b3("CH", slice(j, None, 4), full), False, j == 3)
+        tt(b("ow1"), CHW, vr, A.is_equal)
+        mm(b("P0", 0, 256), b("PAR"), b("ow1"))
+        tt(b("FK"), b("Fl"), b("P2", 0, 256), A.mult)
+        vtr(b3("R4"), b3("Q0", slice(0, 4), full))
+        cp(b3("ci"), b3("R4", full, slice(0, 8)))
+        ts(b("iv"), b3("R4", full, slice(8, 12)), 0.0, 8.0, A.is_gt, A.mult)
+        ts(b3("ca"), b3("ci"), 4095, None, A.bitwise_and)
+        tt(b("iv2"), b("iv"), b("dm8"), A.max)
+        tt(b("ch"), b3("ca", full, slice(0, 8, 2)), b3("ca", full, slice(1, 8, 2)), A.mult)
+        tt(b("cc"), b("FK"), b("P0", 0, 256), A.mult)
+        ts(b("ow"), b("ch"), 5, 7, A.arith_shift_right, A.bitwise_and)
+        tt(b("PK"), b("cc"), CHW, A.add)
+        tt(b("own"), b("ow"), b("iv2"), A.add)
+        for o in range(9):
+            ts(b("O", 16 * o, 16 * o + 16), b("own"), float(o), None, A.is_equal if o < 8 else A.is_ge)
+        mm(b("P3", 0, 144), b("BH"), b("O"))
+        mm(b("P5", 0, 144), b("NU"), b("O"), True, False)
+        mm(b("P5", 0, 144), b("e0h"), b("c9"), False, True)
+        scan(b("I9"), b("m16", 0, 144), b("P3", 0, 144), A.mult, A.add)
+        tt(b("A9"), b("I9"), b("P5", 0, 144), A.add)
+        tt(b("s9"), b("A9"), b("O"), A.mult)
+        tt(b("t64"), b("s9", 0, 64), b("s9", 64, 128), A.add)
+        tt(b("t32"), b("t64", 0, 32), b("t64", 32, 64), A.add)
+        tt(b("t16"), b("t32", 0, 16), b("s9", 128, 144), A.add)
+        tt(b("slf"), b("t16"), b("t32", 16, 32), A.add)
+        cp(b("slu"), b("slf"))
+        SL, LA = "SL%d" % t, "LA%d" % t
+        cp(ind(b(SL), b("slu")), b("PK"))
+        for call in (0, 1):
+            tr = []
+            for cl, d, eng in plan[core]:
+                if cl != call:
+                    continue
+                o, at = T.rank_of(d), CAP * land[d].index(me)
+                need("g", b(SL, 256 * o, 256 * o + CAP)[1], [])
+                tr.append(RemoteDMATransfer(
+                    dst_ids=[DstId(rid=topo.addr(d)[0], pnc=topo.addr(d)[1])], dma_engine_mask=sum(1 << e for e in eng),
+                    remote_sem=T.sem[("an%d" if topo.chip(d) == topo.chip(core) else "ar%d") % t],
+                    src=T[SL][:, 256 * o:256 * o + CAP], dst=T[LA][:, at:at + CAP]))
+                sent[0] += len(eng)
+            g.remote_dma_fused(tr, local_sem=T.sem.loc)
+        for d in T.cores:
+            if d != core:
+                nr = topo.chip(d) == topo.chip(core)
+                tot = sum(len(e) for s in T.cores if s != core and (topo.chip(s) == topo.chip(core)) == nr
+                          for _, x, e in plan[s] if x == core)
+                at = CAP * land[core].index(T.rank_of(d))
+                acc.setdefault(LA, []).append((at, at + CAP, 1, ("an%d" if nr else "ar%d") % t, tot, "r"))
+        at = CAP * land[core].index(me)
+        cp(b(LA, at, at + CAP), b(SL, 256 * me, 256 * me + CAP))
+        if t == 0:
+            arrival_constants()
+        act(b("P0", 0, 256), b("C"), F.Sign)
+        act(b("P1", 0, 256), b("T6"), F.Identity, bias=128.0)
+        tt(b("Cf"), b("C"), b("P0", 0, 256), A.subtract)
+        act(b("fsq"), b("Cf"), F.Square)
+        mm(b("P2", 0, 256), b("BB"), b("fsq"))
+        act(b("fsg"), b("P2", 0, 256), F.Sign, bias=-0.5)
+        mm(b("P3", 0, 256), b("AL"), b("fsg"))
+        tt(b("fo"), b("pl"), b("dtr", 0, 16), A.add)
+        tt(b("xf"), b("Cf"), b("P1", 0, 256), A.add)
+        tt(b("fo2"), b("fo"), b("vw"), A.mult)
+        tt(b("fo3"), b("fo2"), b("sw", 0, 16), A.add)
+        cp(b("fou"), b("fo3"))
+        tt(b("xg"), b("xf"), b("P3", 0, 256), A.add)
+        cp(ind(b("X"), b("fou")), b("xg"))
+
+        def score(bank, lo):
+            q = (lo, lo + 60)
+            ts(b("k1", *q), b(bank, 0, 60), 0.0, None, A.is_equal)
+            act(b("k2", *q), b(bank, 0, 60), F.Sign, bias=-THETA)
+            mm(b("P4", *q), b("e0b"), b("kcm", *q), True, False)
+            mm(b("P4", *q), b("ID32"), b("k1", *q), False, False)
+            mm(b("P4", *q), b("ID8"), b("k2", *q), False, True)
+
+        def arrivals(part):
+            c0, c2 = PART[part]
+            w = c2 - c0
+            wp, n, ways = w + 1, 16 * w, w // 5
+            a0, z0 = 16 * c0, 960 * part
+            A16 = b3("A16", slice(c0, c2), full)
+            ts(A16, b(LA, a0, a0 + n), M23, -M23, A.add, A.add)
+            for par, nh in ((0, "EH"), (16, "OH")):
+                for j in range(ways):
+                    mm(b3("Q1p", slice(0, 5), slice(par, par + 16)), b(nh, 6 - 2 * j, 134 - 2 * j),
+                       b3("A16", slice(c0 + j, c2, ways), full), j == 0, j == ways - 1)
+            ts(b("Q1", a0, a0 + n), A16, 256.0, 524288.0 + OFF - M31, A.mult, A.add)
+            vtr(b3("R5"), b3("Q1p", slice(0, 5), full))
+            cp(b3("ai5", full, slice(0, 2 * ways)), b3("R5", full, slice(0, 2 * ways)))
+            ts(b3("aa5", full, slice(0, 2 * ways)), b3("ai5", full, slice(0, 2 * ways)), 4095, None, A.bitwise_and)
+            u1, u2 = b3("aa5", full, slice(0, 2 * ways, 2)), b3("aa5", full, slice(1, 2 * ways, 2))
+            s0 = 6 * part
+            st = b("st", s0, s0 + wp)
+            ts(b("st", s0, s0 + w), u1, 2.0, 1.0, A.mult, A.add)
+            tt(b("ah", 0, w), u1, u2, A.mult)
+            act(b("s2", 0, wp), st, F.Copy, scale=2.0)
+            act(b("s2", wp, 2 * wp), st, F.Copy, scale=2.0)
+            act(b("s4", 0, 2 * wp), b("s2", 0, 2 * wp), F.Copy, scale=2.0)
+            act(b("s4", 2 * wp, 4 * wp), b("s2", 0, 2 * wp), F.Copy, scale=2.0)
+            act(b("s8", 0, 4 * wp), b("s4", 0, 4 * wp), F.Copy, scale=2.0)
+            ts(b("Z", 0, w), b("ah", 0, w), 8, V - 1, A.arith_shift_right, A.bitwise_and)
+            tt(b("Z", wp, 2 * wp), b("Z", 0, wp), st, A.add)
+            ts(b("Hh", c0, c2), b("ah", 0, w), 8, V - 1, A.arith_shift_right, A.bitwise_and)
+            tt(b("Z", 2 * wp, 4 * wp), b("Z", 0, 2 * wp), b("s2", 0, 2 * wp), A.add)
+            ts(b("Zm", 0, 4 * wp), b("Z", 0, 4 * wp), V - 1, None, A.bitwise_and)
+            cp(b("zu", 0, 4 * wp), b("Zm", 0, 4 * wp))
+            for m in range(NP):
+                if m == 1:
+                    tt(b("Z", 4 * wp, 8 * wp), b("Z", 0, 4 * wp), b("s4", 0, 4 * wp), A.add)
+                    tt(b("Z", 8 * wp, 12 * wp), b("Z", 0, 4 * wp), b("s8", 0, 4 * wp), A.add)
+                    ts(b("Zm", 4 * wp, 12 * wp), b("Z", 4 * wp, 12 * wp), V - 1, None, A.bitwise_and)
+                    cp(b("zu", 4 * wp, 12 * wp), b("Zm", 4 * wp, 12 * wp))
+                d = (z0 + n * m, z0 + n * m + n)
+                tt(b("dd", *d), ind(XW, b("zu", wp * m, wp * m + w)), b("Q1", a0, a0 + n), A.subtract)
+                if part or m % 4 == 3:
+                    d = d if part else (z0 + n * (m - 3), z0 + n * m + n)
+                    act(b("sq", *d), b("dd", *d), F.Square, bias=-M31 / 256.0, scale=1.0 / 256.0)
+                if part and m % 4 == 3 or m == NP - 1:
+                    k = m // 4 + 1 if part else 0
+                    for x in range(16):
+                        mm(b("P%d" % k, 0, 60), b("ZS", 15 - x, 143 - x), b("sq", 960 * k + x, 960 * k + 960, 16), x == 0, x == 15)
+                    if k > 1:
+                        score("P%d" % (k - 1), 60 * (k - 1))
+                    if k == 2:
+                        act(b("KS"), b("P4", 60, 120), F.Copy)
+
+        arrivals(0)
+        if t == RO - 1:
+            for k in range(4):
+                q = (TR + 512 * k, TR + 512 * k + 512)
+                act(b("SG", *q4(k)), b("X", *q), F.Sign)
+                mm(b("P%d" % (1 + k)), b("AL"), b("SG", *q4(k)))
+                tt(b("Y", *q), b("X", *q), b("P%d" % (1 + k)), A.subtract)
+        score("P0", 0)
+        act(b("K3", 0, 30), b("P4", 0, 30), F.Copy)
+        tt(b("K2", 0, 30), b("K3", 0, 30), b("P4", 30, 60), A.max)
+        tt(b("K1", 0, 15), b("K2", 0, 15), b("K2", 15, 30), A.max)
+        tt(b("K2", 0, 5), b("K1", 0, 5), b("K1", 5, 10), A.max)
+        tt(b("km", 0, 5), b("K2", 0, 5), b("K1", 10, 15), A.max)
+        arrivals(1)
+        A16 = b3("A16")
+        tt(b("ac"), b(LA), A16, A.subtract)
+        ts(b("xk"), A16, 256.0, 524288.0 + 128.0, A.mult, A.add)
+        act(b("cq"), b("ac"), F.Copy, scale=256.0)
+        score("P3", 180)
+        tt(b("K1"), b("KS"), b("P4", 120, 180), A.max)
+        tt(b("K2"), b("K1"), b("P4", 180, 240), A.max)
+        tt(b("K3", 0, 30), b("K2", 0, 30), b("K2", 30, 60), A.max)
+        tt(b("km", 5, 20), b("K3", 0, 15), b("K3", 15, 30), A.max)
+        ts(b("mi"), b("km"), -1.0, None, A.mult)
+        ts(b("va"), b("km"), 0.0, None, A.is_gt)
+        ts(b("ma"), b("mi"), 15, None, A.bitwise_and)
+        tt(b("ms", 0, 5), b("ma", 0, 5), b("st", 0, 5), A.mult)
+        tt(b("ms", 5, 20), b("ma", 5, 20), b("st", 6, 21), A.mult)
+        tt(b("pz"), b("ms"), b("Hh"), A.add)
+        ts(b("pm"), b("pz"), V - 1, None, A.bitwise_and)
+        cp(b("pu"), b("pm"))
+        ts(b("pv"), b("pm"), 1.0, None, A.add)
+        tt(b("dp"), b("pv"), b("va"), A.mult)
+        ts(b("pvh"), b("dp"), -1.0, None, A.add)
+        for x in range(16):
+            mm(b("P5", x, AR, 16), b("RX", 128 * x, 128 * x + 128), b("pvh"))
+        mm(b("P0", 0, AR), b("ID"), b("CM"), True, False)
+        for x in range(16):
+            mm(b("P0", x, AR, 16), b("ID"), b("pvh"), False, x == 15)
+        act(b("xm"), ind(XW, b("pu")), F.Identity, bias=M31)
+        act(b("P1", 0, AR), b("xm"), F.Identity, bias=-M31)
+        tt(b("w1"), ind(XW, b("pu")), b("cq"), A.add)
+        ts(b("pv"), b("dp"), -1.0, None, A.add)
+        cp(b("Pr"), b("P5", 0, AR))
+        o5 = own0 // near * PART[0][1]
+        n5 = PART[0][1]
+        rng = []
+        for k in range(20):
+            r = [(0, k), (n5, n5 + o5)] if k < n5 else [(n5 if k < n5 + o5 else 0, k)]
+            rng.append((sum(y - x for x, y in r), k, [(x, y) for x, y in r if x < y]))
+        at, small = 0, []
+        for size, k, rs in sorted(rng, reverse=True):
+            if not size:
+                continue
+            e0 = at
+            for x, y in rs:
+                ts(b("EQ", at, at + 16 * (y - x)), b("Pr", 16 * x, 16 * y), b("pv", k, k + 1), None, A.is_equal)
+                at += 16 * (y - x)
+            if size > 8:
+                act(b("jnk", 0, at - e0), b("EQ", e0, at), F.Copy, accum=b("lw", k, k + 1))
+            else:
+                small.append((k, e0, at))
+        tt(b("DG"), b("Pr"), b("P0", 0, AR), A.is_equal)
+        tt(b("cn"), b("w1"), b("P1", 0, AR), A.subtract)
+        for k, e0, e2 in small:
+            red(b("lw", k, k + 1), b("EQ", e0, e2), A.add)
+        ts(b("ck"), b("cn"), 127.0, -127.0, A.min, A.max)
+        scan(b("DS"), b("m16b"), b("DG"), A.mult, A.max)
+        tt(b("dp"), b("pm"), b("dtr"), A.add)
+        tt(b("xn"), b("xk"), b("ck"), A.add)
+        tt(b("dp2"), b("dp"), b("va"), A.mult)
+        if t < RO - 1:
+            act(b("esq"), b("ck"), F.Square)
+            mm(b("P3", 0, AR), b("BB"), b("esq"))
+            act(b("esg"), b("P3", 0, AR), F.Sign, bias=-0.5)
+            mm(b("P4", 0, AR), b("AL"), b("esg"))
+        tt(b("l2"), b("lw"), b("DS", 15, AR, 16), A.add)
+        ts(b("wn"), b("l2"), 0.0, None, A.is_equal)
+        tt(b("eo"), b("wn"), b("dp2"), A.mult)
+        tt(b("eo2"), b("eo"), b("sw"), A.add)
+        cp(b("eou"), b("eo2"))
+        if t < RO - 1:
+            tt(b("xo"), b("xn"), b("P4", 0, AR), A.add)
+            cp(ind(b("X"), b("eou")), b("xo"))
+        else:
+            cp(ind(b("Y"), b("eou")), b("xn"))
+    for k, e in ((0, "y"), (1, "s")):
+        dma(e, (T.y[:, 1024 * k:1024 * k + 1024], []), b("Y", TR + 1024 * k, TR + 1024 * k + 1024), "d%d" % (5 + k))
+    for s in ("sv", "ss", "sp", "sg"):
+        g.wait_ge(T.sem[s], cnt[s])
+    for k in range(7):
+        g.wait_ge(T.sem["d%d" % k], 16)
+    g.wait_ge(T.sem.loc, sent[0])

@@ -13,19 +13,18 @@ THETA = 1.14e10
 
 _DT = {"f": "float32", "b": "bfloat16", "h": "float16", "i": "int32", "u": "uint16"}
 _SBUF = """
-f X:2368 Y:2368 J:256 JI:128 JG:128 PD:128 jm6:144 jm15:144 jm11:144 tm:144 tm2:144 col:32 ones:128 sw:20 swj:16 swp:16 swh:16 Jp:256
-f dtr:20 c9f:144 m16:256 MX:16 E:128 U:136 acs:16 acv:16 cb:16 vw:16 dm8:16 fo:16 fo2:16 fo3:16 T6:256 Sx:256 C:256 Ks:256 hb:16
-f rk:16 VK:512 R1:256 R2:256 m1:256 FK:256 cc:256 PK:256 iv:16 iv2:16 own:16 I9:144 A9:144 s9:144 t64:64 t32:32 t16:16 slf:16
+f X:2368 Y:2368 J:256 JI:128 JG:128 PD:128 jm6:144 jm15:144 jm11:144 tm:144 tm2:144 tm3:144 tm4:144 col:32 ones:128 sw:20 swh:16
+f Jp:256 dtr:20 c9f:144 m16:256 MX:16 E:128 U:136 acc:16 cb:16 vw:16 dm8:16 fo:16 fo2:16 fo3:16 T6:256 Sx:256 C:256 Ks:256 hb:16
+f rk:16 VK:512 R1:256 R2:256 m1:256 FK:256 cc:256 PK:256 iv:16 iv2:16 own:16 I9:144 A9:144 plS:20 swS:20 t1:20 t2:20 t3:20 iv3:20
 f SL0:2304 SL1:2304 LA0:320 LA1:320 Cf:256 xf:256 xg:256 Q1:320 ac:320 st:24 s2:32 s4:64 s8:64 dd:3840 KS:60 K1:60 K2:60 K3:32
-f km:20 ms:20 va:20 pv:20 dp:20 dp2:20 lw:20 l2:20 wn:20 eo:20 eo2:20 w1:320 xm:320 xk:320 cn:320 ck:320 cq:320 xn:320 xo:320
-f R4:4,32 R5:5,32
-i XI:2048 X1:2048 pp_i:1 pq_i:1 ai:16 pl:16 hp:16 hq:16 vi:16 vv:16 Fl:256 ch:16 ow:16 ah:16 Hh:20 Z:192 Zm:192 mi:20 ma:20 pz:20 pm:20
+f ms:20 pv:20 lw:20 w1:320 xm:320 cn:320 ck:320 cq:320 xn:320 xo:320 R4:4,32 R5:5,32
+i XI:2048 X1:2048 pp_i:1 pq_i:1 ai:16 pl:16 hp:16 hq:16 vi:16 vv:16 Fl:256 ch:16 ow:16 ah:16 Hh:20 Z:192 Zm:192 km:20 ma:20 pz:20 pm:20
 i hi:2,16 ha:2,16 ci:4,8 ca:4,8 ai5:5,8 aa5:5,8
 h NZ:2048 BH:128 NU:128 SU:128 SD:128 ID:128 BI:128 PAR:128 PK1:128 PK2:128 WT:16 EH:144 OH:144 E1:144 O1:144 e0h:128 RX:2048 CM:320
-h c9:144 Lb:128 G:256 Dh:256 VB:512 mA:256 mB:256 ow1:256 O:144 pvh:20 Pr:320
+h c9:144 s9:144 Lb:128 G:256 Dh:256 VB:512 mA:256 mB:256 ow1:256 O:144 pvh:20 Pr:320
 h CH:16,16 eq:16,16 A16:20,16
-b HM:4096 SG:2064 BB:128 AL:128 ZS:144 I592:8 e0b:128 kc:128 kcm:240 ID32:128 ID8:128 m16b:320 cmp:1024 jnk:2048 Lg:4096 Mn:4096
-b fsq:256 fsg:256 sq:3840 k1:240 k2:240 EQ:3040 DG:320 DS:320 esq:320 esg:320
+b HM:4096 SG:2064 SR:2048 BB:128 AL:128 ZS:144 I592:8 e0b:128 kc:128 kcm:240 ID32:128 ID8:128 m16b:320 cmp:1040 jnk:3040 Lg:4096
+b Mn:4096 fsq:256 fsg:256 sq:3840 k1:240 k2:240 EQ:3040 DG:320 DS:320 esq:320 esg:320
 u cu:16 plu:16 fou:16 Du:256 slu:16 zu:256 pu:20 eou:20
 """
 _ALL, SCRATCH, _AT = {}, {}, {}
@@ -60,7 +59,7 @@ def routes(src, T, topo):
     n = len(eng)
     out = [(0, d, eng[k * n // 4:(k + 1) * n // 4]) for k, d in enumerate(far[:4])]
     out += [(1, d, eng[k * n // 2:(k + 1) * n // 2]) for k, d in enumerate(far[4:])]
-    return out + [(0, d, [e for e in topo.engines(src, d) if e not in eng]) for d in near]
+    return out + [(0, d, [e for e in topo.engines(src, d) if e not in eng][:4]) for d in near]
 
 
 def landing(dst, T, topo):
@@ -181,6 +180,9 @@ def rank_program(g, core, T, topo):
         else:
             op("g", lambda: g.iota(out[0], pat, base, cm, allow_small_or_imprecise_dtypes=True), [out], [])
 
+    def gsel(out, in_):
+        op("g", lambda: g.affine_select(out[0], in_[0], [[0, 8], [1, 16]], A.is_gt, 0.0, 0, 0), [out], [in_])
+
     for k in range(4):
         dma("y", b("XI", 512 * k, 512 * k + 512), (T.det[:, 512 * k:512 * k + 512], []), "d%d" % k)
     dma("s", b("HM"), (T.ham[:], []), "d4")
@@ -190,27 +192,30 @@ def rank_program(g, core, T, topo):
     iota("jm15", [[1, 144]], -15, 0)
     iota("JI", [[0, 8], [1, 16]], 0, 0)
     iota("PD", [[1, 128]], 0, -1)
-    iota("swj", [[16, 4], [64, 4]], 0, 0)
     iota("J", [[1, 256]], 0, 0)
     iota("jm11", [[1, 144]], -11, 0)
     iota("ones", [[0, 128]], 1, 0)
+    for k in range(6):
+        iota("cmp", [[0, 1]], 128, 0, 144 * k + 128, 144 * k + 129)
     iota("U", [[0, 8]], -1, 0, 128, 136)
     iota("Jp", [[16, 4], [64, 4], [1, 16]], 0, 0)
     iota("jm6", [[1, 144]], -6, 0)
-    iota("c9f", [[256, 9], [0, 16]], -1, 0)
+    iota("c9f", [[256, 9], [0, 16]], -1025, 0)
+    for h in (0, 128):
+        gsel(b("m16", h, h + 128), b("ones"))
     iota("VK", [[0, 512]], 0, 0)
     for o in range(N):
         iota("SL0", [[0, CAP]], SENT, 0, 256 * o, 256 * o + CAP)
-    iota("kcm", [[-1, 12], [0, 5]], 8, 0, 0, 60)
-    iota("kcm", [[-1, 12], [0, 15]], 8, 0, 60, 240)
+    iota("kcm", [[1, 12], [0, 5]], -8, 0, 0, 60)
+    iota("kcm", [[1, 12], [0, 15]], -8, 0, 60, 240)
     iota("lw", [[0, 20]], 0, 0)
     iota("st", [[0, 24]], 0, 0)
     iota("Z", [[0, 192]], 0, 0)
     for o in range(N):
         iota("SL1", [[0, CAP]], SENT, 0, 256 * o, 256 * o + CAP)
 
-    PI, PG16, PGE, PGO, IM, ACOL, BCOL, W1, W2, SIG, WAL, P0C, PGE1, PGO1, SIGK, SIGM, E0C, N15, OD, PP, N0 = \
-        [b("col", k, k + 1) for k in range(21)]
+    PI, PG16, PGE, PGO, IM, ACOL, BCOL, W1, W2, SIG, WAL, P0C, PGE1, PGO1, SIGK, SIGM, E0C, N15, OD, N0 = \
+        [b("col", k, k + 1) for k in range(20)]
     q_i = b("pq_i")
     ts(q_i, b("pp_i"), 15, None, A.bitwise_and)
     ts(PI, q_i, 1.0, None, A.mult)
@@ -233,61 +238,66 @@ def rank_program(g, core, T, topo):
     ts(b("E1"), b("jm11"), PGE, None, A.is_equal)
     ts(b("O1"), b("jm11"), PGO, None, A.is_equal)
     ts(b("sw"), b("J", 0, 20), 16.0, PI, A.mult, A.add)
-    ts(b("swp"), b("swj"), PI, None, A.add)
-    ts(b("swh"), b("swp"), 0.5, None, A.add)
+    ts(b("swh"), b("sw", 0, 16), 0.5, None, A.add)
 
     def spawn_constants():
-        ts(b("ID"), b("PD"), 0.0, None, A.is_equal)
+        ts(q_i, b("pp_i"), 1, None, A.bitwise_and)
         ts(W1, PI, 13.0, 5.0, A.mult, A.add)
         ts(W2, PI, -14.0, 255.0, A.mult, A.add)
         ts(P0C, b("pp_i"), 0.0, None, A.is_equal)
+        ts(SIG, q_i, -2.0, 1.0, A.mult, A.add)
+        ts(IM, PI, -7.5, None, A.add)
+        ts(N0, PI, 0.0, None, A.is_gt)
+        ts(N15, PI, 15.0, None, A.is_lt)
+        ts(SIGK, SIG, 1.0 / 256.0, None, A.mult)
+        ts(SIGM, SIG, -1.0 / 256.0, None, A.mult)
+        ts(PGE1, PGE, 1.0, None, A.add)
+        ts(PGO1, PGO, 1.0, None, A.add)
         ts(b("WT", 0, 8), b("BH", 0, 128, 16), W1, None, A.mult)
         ts(b("WT", 8, 16), b("BH", 0, 128, 16), W2, None, A.mult)
         ts(b("e0b"), b("J", 0, 128), 0.0, P0C, A.mult, A.add)
         ts(b("kc"), b("JI"), -1.0, 7.5, A.mult, A.add)
         ts(b("I592"), b("BH", 0, 128, 16), 592.0, None, A.mult)
-        ts(b("m16", 0, 128), b("JI"), 0.0, None, A.is_gt)
-        cp(b("m16", 128, 256), b("m16", 0, 128))
-        ts(IM, PI, -7.5, None, A.add)
-        ts(N0, PI, 0.0, None, A.is_gt)
-        ts(N15, PI, 15.0, None, A.is_lt)
         ts(ACOL, N15, -1.0, None, A.mult)
         ts(BCOL, N0, -1.0, None, A.add)
+        ts(b("dtr"), b("sw"), -1.0, float(TR), A.mult, A.add)
+        ts(b("ID"), b("PD"), 0.0, None, A.is_equal)
         ts(b("SU"), b("PD"), -1.0, N0, A.is_equal, A.mult)
         ts(b("SD"), b("PD"), 1.0, N15, A.is_equal, A.mult)
         ts(b("BI"), b("PD"), 0.0, 8192.0, A.is_equal, A.mult)
-        ts(q_i, b("pp_i"), 1, None, A.bitwise_and)
-        ts(SIG, q_i, -2.0, 1.0, A.mult, A.add)
-        ts(SIGK, SIG, 1.0 / 256.0, None, A.mult)
-        ts(SIGM, SIG, -1.0 / 256.0, None, A.mult)
+
+    def child_constants():
+        ts(b("tm2"), b("jm6"), PGE, W1, A.is_equal, A.mult)
+        ts(b("tm"), b("jm6"), PGE1, W2, A.is_equal, A.mult)
+        ts(b("tm3"), b("jm6"), PGO, W1, A.is_equal, A.mult)
+        ts(b("tm4"), b("jm6"), PGO1, W2, A.is_equal, A.mult)
         ts(b("PAR"), b("BH"), SIG, None, A.mult)
+        tt(b("EH"), b("tm"), b("tm2"), A.add)
+        tt(b("OH"), b("tm3"), b("tm4"), A.add)
         ts(b("PK1"), b("BH"), SIGK, None, A.mult)
         ts(b("PK2"), b("BH"), SIGM, None, A.mult)
-        ts(PGE1, PGE, 1.0, None, A.add)
-        ts(PGO1, PGO, 1.0, None, A.add)
-        for n, c0, c1 in (("EH", PGE, PGE1), ("OH", PGO, PGO1)):
-            ts(b("tm2"), b("jm6"), c0, W1, A.is_equal, A.mult)
-            ts(b("tm"), b("jm6"), c1, W2, A.is_equal, A.mult)
-            tt(b(n), b("tm"), b("tm2"), A.add)
+        cp(b("BB"), b("BH"))
         cp(b("e0h"), b("e0b"))
         cp(b("c9"), b("c9f"))
 
     def arrival_constants():
-        cp(b("BB"), b("BH"))
-        ts(b("ID32"), b("ID"), 32.0, None, A.mult)
-        ts(b("ID8"), b("ID"), 8.0, None, A.mult)
+        ts(b("ID32"), b("ID"), -32.0, None, A.mult)
+        ts(b("ID8"), b("ID"), -8.0, None, A.mult)
         ts(b("MX"), b("J", 0, 16), PI, None, A.is_equal)
-        for x in range(16):
-            ts(b("RX", 128 * x, 128 * x + 128), b("BH"), b("MX", x, x + 1), None, A.mult)
         for lo, hi in ((0, 128), (128, 256), (256, 320)):
             ts(b("CM", lo, hi), b("JI", 0, hi - lo), PI, 0.5, A.is_ge, A.mult)
             cp(b("m16b", lo, hi), b("m16", 0, hi - lo))
-        ts(b("dtr"), b("sw"), -1.0, float(TR), A.mult, A.add)
+        ts(b("swS"), b("sw"), 1.0 / 65536.0, None, A.mult)
+        for x in range(16):
+            ts(b("RX", 128 * x, 128 * x + 128), b("BH"), b("MX", x, x + 1), None, A.mult)
 
     def q4(k):
         return 512 * k, 512 * k + 512
     for k in range(4):
-        ts(b("X1", *q4(k)), b("XI", *q4(k)), 255, None, A.bitwise_and)
+        if k == 0:
+            ts(b("X1", *q4(0)), b("XI", *q4(0)), 255, None, A.bitwise_and)
+        if k < 3:
+            ts(b("X1", *q4(k + 1)), b("XI", *q4(k + 1)), 255, None, A.bitwise_and)
         ts(b("NZ", *q4(k)), b("X1", *q4(k)), 128.0, None, A.not_equal)
         mm(b("P%d" % k), b("BH"), b("NZ", *q4(k)))
         act(b("SG", *q4(k)), b("P%d" % k), F.Sign, bias=-0.5)
@@ -306,21 +316,22 @@ def rank_program(g, core, T, topo):
     for t in range(RO):
         start = STEP * (t + 1)
         if t:
-            for k in range(4):
-                x = b("X", TR + 512 * k, TR + 512 * k + 512)
+            for k, (lo, hi) in enumerate(((0, V - start), (512, 1024), (V - start, 512), (1536, V), (1024, 1536))):
+                x = b("X", TR + (lo + start) % V, TR + (hi - 1 + start) % V + 1)
                 if k % 2:
-                    ts(b("SG", *q4(k)), x, 0.0, None, A.is_gt)
+                    act(b("SR", lo, hi), x, F.Sign)
                 else:
-                    act(b("SG", *q4(k)), x, F.Sign)
-                    if k == 0:
-                        act(b("SG", V, V + 16), b("X", TR, TR + 16), F.Sign)
-        c1 = (V - start + 15) // 16
-        e1 = start + 16 * c1 - V
-        for x in range(16):
-            mm(b("P4", 0, c1), b("ZS", 15 - x, 143 - x), b("SG", start + x, start + x + 16 * (c1 - 1) + 1, 16), x == 0, x == 15)
-        for x in range(16):
-            mm(b("P4", c1, 128), b("ZS", 15 - x, 143 - x), b("SG", e1 + x, e1 + x + 16 * (127 - c1) + 1, 16), x == 0, x == 15)
-        if t == 0:
+                    ts(b("SR", lo, hi), x, 0.0, None, A.is_gt)
+            for h in (0, 64):
+                for x in range(16):
+                    mm(b("P4", h, h + 64), b("ZS", 15 - x, 143 - x), b("SR", 16 * h + x, 16 * h + 1024, 16), x == 0, x == 15)
+        else:
+            c1 = (V - start + 15) // 16
+            e1 = start + 16 * c1 - V
+            for x in range(16):
+                mm(b("P4", 0, c1), b("ZS", 15 - x, 143 - x), b("SG", start + x, start + x + 16 * (c1 - 1) + 1, 16), x == 0, x == 15)
+            for x in range(16):
+                mm(b("P4", c1, 128), b("ZS", 15 - x, 143 - x), b("SG", e1 + x, e1 + x + 16 * (127 - c1) + 1, 16), x == 0, x == 15)
             spawn_constants()
         ts(b("Lb"), b("P4", 0, 128), 0.0, None, A.is_gt)
         mm(b("P5", 0, 128), b("BH"), b("Lb"))
@@ -331,22 +342,19 @@ def rank_program(g, core, T, topo):
         scan(b("E"), b("ones"), b("P5", 0, 128), A.mult, A.add)
         NA = 10
         for k in range(NA):
-            act(b("jnk", 128 * k, 128 * k + 128), b("E"), F.Sign, bias=b("swh", k, k + 1), scale=-1.0, accum=b("acs", k, k + 1))
+            act(b("jnk", 128 * k, 128 * k + 128), b("E"), F.Sign, bias=b("swh", k, k + 1), scale=-1.0, accum=b("acc", k, k + 1))
         tt(b("U", 0, 128), b("E"), b("P4", 128, 256), A.add)
         for k in range(NA, 17):
+            o = 144 * (k - NA)
             if k < 16:
-                ts(b("cmp", 128 * (k - NA), 128 * (k - NA) + 128), b("E"), b("swp", k, k + 1), None, A.is_le)
+                ts(b("cmp", o, o + 128), b("E"), b("sw", k, k + 1), -2.0, A.is_gt, A.mult)
             if k > NA:
-                red(b("acv", k - 1, k), b("cmp", 128 * (k - 1 - NA), 128 * (k - NA)), A.add)
+                red(b("acc", k - 1, k), b("cmp", o - 144, o - 15), A.add)
         ts(b("vw"), b("sw", 0, 16), b("E", 127, 128), None, A.is_lt)
-        ts(b("cu", NA, 16), b("acv", NA, 16), 1.0, None, A.mult)
-        ts(b("cu", 0, NA), b("acs", 0, NA), 0.5, 64.0, A.mult, A.add)
+        for j in range(4):
+            ts(b("cu", 4 * j, 4 * j + 4), b("acc", j, 16, 4), 0.5, 64.0, A.mult, A.add)
         tt(b("G"), ind(b("U"), b("cu")), b("Jp"), A.is_le)
-        for lo, hi, n, sl, bi in ((0, NA, "acs", 8.0, 1024.0), (NA, 16, "acv", 16.0, 0.0)):
-            for j in range(4):
-                u0, u1 = max(lo, 4 * j), min(hi, 4 * j + 4)
-                if u0 < u1:
-                    ts(b("cb", j + 4 * (u0 - 4 * j), j + 4 * (u1 - 1 - 4 * j) + 1, 4), b(n, u0, u1), sl, bi + start, A.mult, A.add)
+        ts(b("cb"), b("acc"), 8.0, 1024.0 + start, A.mult, A.add)
         ts(b("dm8"), b("vw"), -8.0, 8.0, A.mult, A.add)
         for par, n in ((0, "E1"), (16, "O1")):
             for j in range(4):
@@ -367,27 +375,46 @@ def rank_program(g, core, T, topo):
                 act(b("P0", 0, 256), b("C"), F.Abs)
             else:
                 act(b("Lg", 16 * lo, 16 * hi), ind(b("HM"), b("Du", lo, hi)), F.Copy)
+        act(b("P4", 0, 256), b("C"), F.Sign)
+        act(b("P5", 0, 256), b("T6"), F.Identity, bias=128.0)
         ts(b("Dh"), b("T6"), 1.0 / 256.0, -2048.0, A.mult, A.add)
+        if t == 0:
+            child_constants()
         cp(b("Lg", 0, 1024), ind(b("HM"), b("Du", 0, 64)))
         for h in range(2):
             mm(b("P3", 16 * h, 16 * h + 16), b("Dh", 128 * h, 128 * h + 128), b("WT"))
         for h in range(2):
             mm(b("P%d" % (1 + h), 0, 128), b("e0b"), b("kc"), True, False)
+
+        def hash_step(k):
+            if k == 0:
+                cp(b3("hi"), b("P3", 0, 32))
+            elif k == 1:
+                ts(b3("ha"), b3("hi"), 4095, None, A.bitwise_and)
+            elif k == 2:
+                tt(b("hp"), b3("ha", full, slice(0, 8)), b3("ha", full, slice(8, 16)), A.mult)
+            elif k == 3:
+                ts(b("hq"), b("hp"), 5, None, A.arith_shift_right)
+            elif k == 4:
+                ts(b("hb"), b("hq"), 16.0, M27 + 16.0 * t, A.mult, A.add)
+            else:
+                ts(b("Fl"), b("C"), 0.25, -0.375, A.mult, A.add)
+
         for qd in range(4):
             lo, h = 64 * qd, qd // 2
             for k in range(16):
                 tt(b("Mn", 256 * k + lo, 256 * k + lo + 64), b("Lg", 16 * lo + k, 16 * lo + 1024, 16), b("P0", lo, lo + 64), A.min)
+                if qd == 1 and k % 2 == 0 and k < 12:
+                    hash_step(k // 2)
                 if qd % 2:
                     mm(b("P%d" % (1 + h), k, 128, 16), b("Mn", 256 * k + 128 * h, 256 * k + 128 * h + 128), b("I592"), False, k == 15)
-            if qd == 1:
-                cp(b3("hi"), b("P3", 0, 32))
-                ts(b("Fl"), b("C"), 0.25, -0.375, A.mult, A.add)
-                ts(b3("ha"), b3("hi"), 4095, None, A.bitwise_and)
-                tt(b("hp"), b3("ha", full, slice(0, 8)), b3("ha", full, slice(8, 16)), A.mult)
-                ts(b("hq"), b("hp"), 5, None, A.arith_shift_right)
-                ts(b("hb"), b("hq"), 16.0, M27 + 16.0 * t, A.mult, A.add)
             if qd == 2:
                 scan(b("Ks", 0, 128), b("m16", 0, 128), b("P1", 0, 128), A.mult, A.max)
+        tt(b("Cf"), b("C"), b("P4", 0, 256), A.subtract)
+        act(b("fsq"), b("Cf"), F.Square)
+        tt(b("xf"), b("Cf"), b("P5", 0, 256), A.add)
+        mm(b("P0", 0, 256), b("BB"), b("fsq"))
+        act(b("fsg"), b("P0", 0, 256), F.Sign, bias=-0.5)
         scan(b("Ks", 128, 256), b("m16", 0, 128), b("P2", 0, 128), A.mult, A.max)
         kmx = b("Ks", 15, 256, 16)
         tt(b("vi"), kmx, b("hb"), A.add)
@@ -397,6 +424,7 @@ def rank_program(g, core, T, topo):
         ts(b("VK", 0, 256, 16), b("vv"), -2048.0, None, A.add)
         scan(b("VB", 256, 512), b("m16"), b("VK", 256, 512), A.mult, A.add)
         scan(b("VB", 0, 256), b("m16"), b("VK", 0, 256), A.mult, A.add)
+        tt(b("fo"), b("pl"), b("dtr", 0, 16), A.add)
         mm(b("P5", 0, 256), b("SU"), b("Dh"), True, False)
         mm(b("P1", 0, 256), b("SD"), b("Dh"), True, False)
         for x in (2, 3, 0, 1):
@@ -408,17 +436,22 @@ def rank_program(g, core, T, topo):
         mm(b("P1", 0, 256), b("BI"), b("mB"), False, True)
         mm(b("P2", 0, 256), b("PK1"), b("mA"), True, False)
         mm(b("P2", 0, 256), b("PK2"), b("mB"), False, True)
-        tt(EQW, b("Dh"), vr, A.is_equal)
+        mm(b("P0", 256, 512), b("AL"), b("fsg"))
+        tt(b("fo2"), b("fo"), b("vw"), A.mult)
         tt(b("R1"), b("Dh"), b("P5", 0, 256), A.max)
-        tt(b("m1"), b("R1"), vr, A.min)
         tt(b("R2"), b("Dh"), b("P1", 0, 256), A.min)
+        tt(b("m1"), b("R1"), vr, A.min)
+        tt(EQW, b("Dh"), vr, A.is_equal)
+        tt(b("fo3"), b("fo2"), b("sw", 0, 16), A.add)
         tt(CHW, b("R2"), b("m1"), A.max)
         for par, ns, nh in ((0, "E1", "EH"), (16, "O1", "OH")):
             for j in range(4):
                 mm(b3("Q0", slice(0, 4), slice(par, par + 16)), b(ns, 3 - j, 131 - j), b3("eq", slice(j, None, 4), full), j == 0, False)
             for j in range(4):
                 mm(b3("Q0", slice(0, 4), slice(par, par + 16)), b(nh, 6 - 2 * j, 134 - 2 * j), b3("CH", slice(j, None, 4), full), False, j == 3)
+        cp(b("fou"), b("fo3"))
         tt(b("ow1"), CHW, vr, A.is_equal)
+        tt(b("xg"), b("xf"), b("P0", 256, 512), A.add)
         mm(b("P0", 0, 256), b("PAR"), b("ow1"))
         tt(b("FK"), b("Fl"), b("P2", 0, 256), A.mult)
         vtr(b3("R4"), b3("Q0", slice(0, 4), full))
@@ -439,11 +472,10 @@ def rank_program(g, core, T, topo):
         scan(b("I9"), b("m16", 0, 144), b("P3", 0, 144), A.mult, A.add)
         tt(b("A9"), b("I9"), b("P5", 0, 144), A.add)
         tt(b("s9"), b("A9"), b("O"), A.mult)
-        tt(b("t64"), b("s9", 0, 64), b("s9", 64, 128), A.add)
-        tt(b("t32"), b("t64", 0, 32), b("t64", 32, 64), A.add)
-        tt(b("t16"), b("t32", 0, 16), b("s9", 128, 144), A.add)
-        tt(b("slf"), b("t16"), b("t32", 16, 32), A.add)
-        cp(b("slu"), b("slf"))
+        for o in range(9):
+            mm(b("P2", 0, 16), b("ID"), b("s9", 16 * o, 16 * o + 16), o == 0, o == 8)
+        cp(ind(b("X"), b("fou")), b("xg"))
+        ts(b("slu"), b("P2", 0, 16), 1024.0, None, A.add)
         SL, LA = "SL%d" % t, "LA%d" % t
         cp(ind(b(SL), b("slu")), b("PK"))
         for call in (0, 1):
@@ -470,20 +502,6 @@ def rank_program(g, core, T, topo):
         cp(b(LA, at, at + CAP), b(SL, 256 * me, 256 * me + CAP))
         if t == 0:
             arrival_constants()
-        act(b("P0", 0, 256), b("C"), F.Sign)
-        act(b("P1", 0, 256), b("T6"), F.Identity, bias=128.0)
-        tt(b("Cf"), b("C"), b("P0", 0, 256), A.subtract)
-        act(b("fsq"), b("Cf"), F.Square)
-        mm(b("P2", 0, 256), b("BB"), b("fsq"))
-        act(b("fsg"), b("P2", 0, 256), F.Sign, bias=-0.5)
-        mm(b("P3", 0, 256), b("AL"), b("fsg"))
-        tt(b("fo"), b("pl"), b("dtr", 0, 16), A.add)
-        tt(b("xf"), b("Cf"), b("P1", 0, 256), A.add)
-        tt(b("fo2"), b("fo"), b("vw"), A.mult)
-        tt(b("fo3"), b("fo2"), b("sw", 0, 16), A.add)
-        cp(b("fou"), b("fo3"))
-        tt(b("xg"), b("xf"), b("P3", 0, 256), A.add)
-        cp(ind(b("X"), b("fou")), b("xg"))
 
         def score(bank, lo):
             q = (lo, lo + 60)
@@ -492,6 +510,23 @@ def rank_program(g, core, T, topo):
             mm(b("P4", *q), b("e0b"), b("kcm", *q), True, False)
             mm(b("P4", *q), b("ID32"), b("k1", *q), False, False)
             mm(b("P4", *q), b("ID8"), b("k2", *q), False, True)
+
+        def sums(k):
+            for x in range(16):
+                mm(b("P%d" % k, 0, 60), b("ZS", 15 - x, 143 - x), b("sq", 960 * k + x, 960 * k + 960, 16), x == 0, x == 15)
+
+        def part0_tail(k):
+            if k == 0:
+                score("P0", 0)
+                act(b("K3", 0, 30), b("P4", 0, 30), F.Copy)
+            elif k == 2:
+                tt(b("K2", 0, 30), b("K3", 0, 30), b("P4", 30, 60), A.min)
+            elif k == 3:
+                tt(b("K1", 0, 15), b("K2", 0, 15), b("K2", 15, 30), A.min)
+            elif k == 4:
+                tt(b("K2", 30, 35), b("K1", 0, 5), b("K1", 5, 10), A.min)
+            elif k == 5:
+                tt(b("km", 0, 5), b("K2", 30, 35), b("K1", 10, 15), A.min)
 
         def arrivals(part):
             c0, c2 = PART[part]
@@ -518,27 +553,47 @@ def rank_program(g, core, T, topo):
             act(b("s4", 0, 2 * wp), b("s2", 0, 2 * wp), F.Copy, scale=2.0)
             act(b("s4", 2 * wp, 4 * wp), b("s2", 0, 2 * wp), F.Copy, scale=2.0)
             act(b("s8", 0, 4 * wp), b("s4", 0, 4 * wp), F.Copy, scale=2.0)
+
+            def zm(lo, hi):
+                ts(b("Zm", lo * wp, hi * wp), b("Z", lo * wp, hi * wp), V - 1, None, A.bitwise_and)
+
+            def zc(lo, hi):
+                cp(b("zu", lo * wp, hi * wp), b("Zm", lo * wp, hi * wp))
+
             ts(b("Z", 0, w), b("ah", 0, w), 8, V - 1, A.arith_shift_right, A.bitwise_and)
-            tt(b("Z", wp, 2 * wp), b("Z", 0, wp), st, A.add)
             ts(b("Hh", c0, c2), b("ah", 0, w), 8, V - 1, A.arith_shift_right, A.bitwise_and)
-            tt(b("Z", 2 * wp, 4 * wp), b("Z", 0, 2 * wp), b("s2", 0, 2 * wp), A.add)
-            ts(b("Zm", 0, 4 * wp), b("Z", 0, 4 * wp), V - 1, None, A.bitwise_and)
-            cp(b("zu", 0, 4 * wp), b("Zm", 0, 4 * wp))
+            cp(b("zu", 0, wp), b("Z", 0, wp))
+            tt(b("Z", wp, 2 * wp), b("Z", 0, wp), st, A.add)
+            if part:
+                sums(0)
+            elif t == RO - 1:
+                for k in range(4):
+                    act(b("SG", *q4(k)), b("X", TR + 512 * k, TR + 512 * k + 512), F.Sign)
+                    mm(b("P%d" % (1 + k)), b("AL"), b("SG", *q4(k)))
             for m in range(NP):
                 if m == 1:
+                    zm(1, 2)
+                    tt(b("Z", 2 * wp, 4 * wp), b("Z", 0, 2 * wp), b("s2", 0, 2 * wp), A.add)
+                    zc(1, 2)
+                    zm(2, 4)
+                if m == 2:
                     tt(b("Z", 4 * wp, 8 * wp), b("Z", 0, 4 * wp), b("s4", 0, 4 * wp), A.add)
+                    zc(2, 4)
                     tt(b("Z", 8 * wp, 12 * wp), b("Z", 0, 4 * wp), b("s8", 0, 4 * wp), A.add)
-                    ts(b("Zm", 4 * wp, 12 * wp), b("Z", 4 * wp, 12 * wp), V - 1, None, A.bitwise_and)
-                    cp(b("zu", 4 * wp, 12 * wp), b("Zm", 4 * wp, 12 * wp))
+                if m == 3:
+                    zm(4, 12)
+                if m == 4:
+                    zc(4, 12)
+                if part and m > 2:
+                    part0_tail(m - 3)
                 d = (z0 + n * m, z0 + n * m + n)
                 tt(b("dd", *d), ind(XW, b("zu", wp * m, wp * m + w)), b("Q1", a0, a0 + n), A.subtract)
                 if part or m % 4 == 3:
                     d = d if part else (z0 + n * (m - 3), z0 + n * m + n)
                     act(b("sq", *d), b("dd", *d), F.Square, bias=-M31 / 256.0, scale=1.0 / 256.0)
-                if part and m % 4 == 3 or m == NP - 1:
-                    k = m // 4 + 1 if part else 0
-                    for x in range(16):
-                        mm(b("P%d" % k, 0, 60), b("ZS", 15 - x, 143 - x), b("sq", 960 * k + x, 960 * k + 960, 16), x == 0, x == 15)
+                if part and m % 4 == 3:
+                    k = m // 4 + 1
+                    sums(k)
                     if k > 1:
                         score("P%d" % (k - 1), 60 * (k - 1))
                     if k == 2:
@@ -548,36 +603,24 @@ def rank_program(g, core, T, topo):
         if t == RO - 1:
             for k in range(4):
                 q = (TR + 512 * k, TR + 512 * k + 512)
-                act(b("SG", *q4(k)), b("X", *q), F.Sign)
-                mm(b("P%d" % (1 + k)), b("AL"), b("SG", *q4(k)))
                 tt(b("Y", *q), b("X", *q), b("P%d" % (1 + k)), A.subtract)
-        score("P0", 0)
-        act(b("K3", 0, 30), b("P4", 0, 30), F.Copy)
-        tt(b("K2", 0, 30), b("K3", 0, 30), b("P4", 30, 60), A.max)
-        tt(b("K1", 0, 15), b("K2", 0, 15), b("K2", 15, 30), A.max)
-        tt(b("K2", 0, 5), b("K1", 0, 5), b("K1", 5, 10), A.max)
-        tt(b("km", 0, 5), b("K2", 0, 5), b("K1", 10, 15), A.max)
         arrivals(1)
-        A16 = b3("A16")
-        tt(b("ac"), b(LA), A16, A.subtract)
-        ts(b("xk"), A16, 256.0, 524288.0 + 128.0, A.mult, A.add)
-        act(b("cq"), b("ac"), F.Copy, scale=256.0)
+        tt(b("ac"), b(LA), b3("A16"), A.subtract)
+        act(b("cq"), b("ac"), F.Identity, bias=128.0, scale=256.0)
         score("P3", 180)
-        tt(b("K1"), b("KS"), b("P4", 120, 180), A.max)
-        tt(b("K2"), b("K1"), b("P4", 180, 240), A.max)
-        tt(b("K3", 0, 30), b("K2", 0, 30), b("K2", 30, 60), A.max)
-        tt(b("km", 5, 20), b("K3", 0, 15), b("K3", 15, 30), A.max)
-        ts(b("mi"), b("km"), -1.0, None, A.mult)
-        ts(b("va"), b("km"), 0.0, None, A.is_gt)
-        ts(b("ma"), b("mi"), 15, None, A.bitwise_and)
+        tt(b("K1"), b("KS"), b("P4", 120, 180), A.min)
+        tt(b("K2"), b("K1"), b("P4", 180, 240), A.min)
+        tt(b("K3", 0, 30), b("K2", 0, 30), b("K2", 30, 60), A.min)
+        tt(b("km", 5, 20), b("K3", 0, 15), b("K3", 15, 30), A.min)
+        ts(b("ma"), b("km"), 15, None, A.bitwise_and)
+        ts(b("iv3"), b("km"), 0.0, -4096.0, A.is_ge, A.mult)
         tt(b("ms", 0, 5), b("ma", 0, 5), b("st", 0, 5), A.mult)
         tt(b("ms", 5, 20), b("ma", 5, 20), b("st", 6, 21), A.mult)
         tt(b("pz"), b("ms"), b("Hh"), A.add)
         ts(b("pm"), b("pz"), V - 1, None, A.bitwise_and)
         cp(b("pu"), b("pm"))
-        ts(b("pv"), b("pm"), 1.0, None, A.add)
-        tt(b("dp"), b("pv"), b("va"), A.mult)
-        ts(b("pvh"), b("dp"), -1.0, None, A.add)
+        tt(b("pvh"), b("pm"), b("iv3"), A.add)
+        tt(b("pv"), b("pm"), b("iv3"), A.add)
         for x in range(16):
             mm(b("P5", x, AR, 16), b("RX", 128 * x, 128 * x + 128), b("pvh"))
         mm(b("P0", 0, AR), b("ID"), b("CM"), True, False)
@@ -586,8 +629,16 @@ def rank_program(g, core, T, topo):
         act(b("xm"), ind(XW, b("pu")), F.Identity, bias=M31)
         act(b("P1", 0, AR), b("xm"), F.Identity, bias=-M31)
         tt(b("w1"), ind(XW, b("pu")), b("cq"), A.add)
-        ts(b("pv"), b("dp"), -1.0, None, A.add)
+        act(b("P2", 0, AR), b("Q1"), F.Identity, bias=M31 - OFF)
+        ts(b("plS"), b("pv"), float(TR), 1.0 / 65536.0, A.add, A.mult)
+        tt(b("cn"), b("w1"), b("P1", 0, AR), A.subtract)
         cp(b("Pr"), b("P5", 0, AR))
+        ts(b("ck"), b("cn"), 255.0, 1.0, A.min, A.max)
+        if t < RO - 1:
+            act(b("esq"), b("ck"), F.Square, bias=-128.0)
+            mm(b("P3", 0, AR), b("BB"), b("esq"))
+            act(b("esg"), b("P3", 0, AR), F.Sign, bias=-0.5)
+            mm(b("P4", 0, AR), b("AL"), b("esg"))
         o5 = own0 // near * PART[0][1]
         n5 = PART[0][1]
         rng = []
@@ -602,31 +653,22 @@ def rank_program(g, core, T, topo):
             for x, y in rs:
                 ts(b("EQ", at, at + 16 * (y - x)), b("Pr", 16 * x, 16 * y), b("pv", k, k + 1), None, A.is_equal)
                 at += 16 * (y - x)
-            if size > 8:
-                act(b("jnk", 0, at - e0), b("EQ", e0, at), F.Copy, accum=b("lw", k, k + 1))
+            if size > 9:
+                act(b("jnk", e0, at), b("EQ", e0, at), F.Copy, accum=b("lw", k, k + 1))
             else:
                 small.append((k, e0, at))
         tt(b("DG"), b("Pr"), b("P0", 0, AR), A.is_equal)
-        tt(b("cn"), b("w1"), b("P1", 0, AR), A.subtract)
         for k, e0, e2 in small:
             red(b("lw", k, k + 1), b("EQ", e0, e2), A.add)
-        ts(b("ck"), b("cn"), 127.0, -127.0, A.min, A.max)
         scan(b("DS"), b("m16b"), b("DG"), A.mult, A.max)
-        tt(b("dp"), b("pm"), b("dtr"), A.add)
-        tt(b("xn"), b("xk"), b("ck"), A.add)
-        tt(b("dp2"), b("dp"), b("va"), A.mult)
-        if t < RO - 1:
-            act(b("esq"), b("ck"), F.Square)
-            mm(b("P3", 0, AR), b("BB"), b("esq"))
-            act(b("esg"), b("P3", 0, AR), F.Sign, bias=-0.5)
-            mm(b("P4", 0, AR), b("AL"), b("esg"))
-        tt(b("l2"), b("lw"), b("DS", 15, AR, 16), A.add)
-        ts(b("wn"), b("l2"), 0.0, None, A.is_equal)
-        tt(b("eo"), b("wn"), b("dp2"), A.mult)
-        tt(b("eo2"), b("eo"), b("sw"), A.add)
-        cp(b("eou"), b("eo2"))
+        tt(b("xn"), b("ck"), b("P2", 0, AR), A.add)
         if t < RO - 1:
             tt(b("xo"), b("xn"), b("P4", 0, AR), A.add)
+        tt(b("t1"), b("plS"), b("DS", 15, AR, 16), A.subtract)
+        tt(b("t2"), b("t1"), b("lw"), A.subtract)
+        tt(b("t3"), b("t2"), b("swS"), A.max)
+        ts(b("eou"), b("t3"), 65536.0, None, A.mult)
+        if t < RO - 1:
             cp(ind(b("X"), b("eou")), b("xo"))
         else:
             cp(ind(b("Y"), b("eou")), b("xn"))

@@ -17,12 +17,12 @@ f X:2368 Y:2368 J:256 JI:128 JG:128 PD:128 jm6:144 jm15:144 jm11:144 tm:144 tm2:
 f Jp:256 dtr:20 c9f:144 m16:256 MX:16 E:128 U:136 acc:16 cb:16 vw:16 dm8:16 fo:16 fo2:16 fo3:16 T6:256 Sx:256 C:256 Ks:256 hb:16
 f rk:16 VK:512 R1:256 R2:256 m1:256 FK:256 cc:256 PK:256 iv:16 iv2:16 own:16 I9:144 A9:144 plS:20 swS:20 t1:20 t2:20 t3:20 iv3:20
 f SL0:2304 SL1:2304 LA0:320 LA1:320 Cf:256 xf:256 xg:256 Q1:320 ac:320 st:24 s2:32 s4:64 s8:64 dd:3840 KS:60 K1:60 K2:60 K3:32
-f ms:20 pv:20 lw:20 w1:320 xm:320 cn:320 ck:320 cq:320 xn:320 xo:320 R4:4,32 R5:5,32
-i XI:2048 X1:2048 pp_i:1 pq_i:1 ai:16 pl:16 hp:16 hq:16 vi:16 vv:16 Fl:256 ch:16 ow:16 ah:16 Hh:20 Z:192 Zm:192 km:20 ma:20 pz:20 pm:20
+f pv:20 lw:20 w1:320 xm:320 cn:320 ck:320 cq:320 xn:320 xo:320 R4:4,32 R5:5,32
+i XI:2048 X1:2048 pp_i:1 pq_i:1 ai:16 pl:16 hp:16 hq:16 vi:16 vv:16 Fl:256 ch:16 ow:16 ah:16 Z:192 Zm:192 km:20 pm:20
 i hi:2,16 ha:2,16 ci:4,8 ca:4,8 ai5:5,8 aa5:5,8
 h NZ:2048 BH:128 NU:128 SU:128 SD:128 ID:128 BI:128 PAR:128 PK1:128 PK2:128 WT:16 EH:144 OH:144 E1:144 O1:144 e0h:128 RX:2048 CM:320
 h c9:144 s9:144 Lb:128 G:256 Dh:256 VB:512 mA:256 mB:256 ow1:256 O:144 pvh:20 Pr:320
-h CH:16,16 eq:16,16 A16:20,16
+h CH:16,16 eq:16,16 A16:20,16 ZH0:12,6 ZH1:12,16
 b HM:4096 SG:2064 SR:2048 BB:128 AL:128 ZS:144 I592:8 e0b:128 kc:128 kcm:240 ID32:128 ID8:128 m16b:320 cmp:1040 jnk:3040 Lg:4096
 b Mn:4096 fsq:256 fsg:256 sq:3840 k1:240 k2:240 EQ:3040 DG:320 DS:320 esq:320 esg:320
 u cu:16 plu:16 fou:16 Du:256 slu:16 zu:256 pu:20 eou:20
@@ -206,8 +206,8 @@ def rank_program(g, core, T, topo):
     iota("VK", [[0, 512]], 0, 0)
     for o in range(N):
         iota("SL0", [[0, CAP]], SENT, 0, 256 * o, 256 * o + CAP)
-    iota("kcm", [[1, 12], [0, 5]], -8, 0, 0, 60)
-    iota("kcm", [[1, 12], [0, 15]], -8, 0, 60, 240)
+    iota("kcm", [[2048, 12], [0, 5]], -16384, 0, 0, 60)
+    iota("kcm", [[2048, 12], [0, 15]], -16384, 0, 60, 240)
     iota("lw", [[0, 20]], 0, 0)
     iota("st", [[0, 24]], 0, 0)
     iota("Z", [[0, 192]], 0, 0)
@@ -223,22 +223,27 @@ def rank_program(g, core, T, topo):
     ts(PG16, q_i, 16.0, None, A.mult)
     ts(OD, q_i, 1.0, None, A.mult)
     ts(b("BH"), b("JG"), OD, None, A.is_equal)
-    ts(b("ZS"), b("jm15"), PG16, None, A.is_equal)
-    ts(E0C, PI, 0.0, OFF, A.is_equal, A.mult)
-    ts(WAL, PI, 1.0, -128.0, A.is_equal, A.mult)
-    tt(WAL, WAL, E0C, A.add)
-    ts(b("AL"), b("BH"), WAL, None, A.mult)
-    ts(b("tm", 0, 128), b("PD"), 0.0, -1.0, A.is_lt, A.mult)
-    tt(b("NU"), b("tm", 0, 128), b("BH"), A.mult)
-    ts(q_i, q_i, 1, None, A.bitwise_and)
-    cp(OD, q_i)
-    ts(PGE, OD, 100000.0, PG16, A.mult, A.add)
-    ts(PGO, OD, -100000.0, 100000.0 - 16.0, A.mult, A.add)
-    tt(PGO, PGO, PG16, A.add)
-    ts(b("E1"), b("jm11"), PGE, None, A.is_equal)
-    ts(b("O1"), b("jm11"), PGO, None, A.is_equal)
-    ts(b("sw"), b("J", 0, 20), 16.0, PI, A.mult, A.add)
-    ts(b("swh"), b("sw", 0, 16), 0.5, None, A.add)
+    fill = [(ts, (b("ZS"), b("jm15"), PG16, None, A.is_equal)),
+            (ts, (E0C, PI, 0.0, OFF, A.is_equal, A.mult)),
+            (ts, (WAL, PI, 1.0, -128.0, A.is_equal, A.mult)),
+            (ts, (b("tm", 0, 128), b("PD"), 0.0, -1.0, A.is_lt, A.mult)),
+            (ts, (b("sw"), b("J", 0, 20), 16.0, PI, A.mult, A.add)),
+            (ts, (q_i, q_i, 1, None, A.bitwise_and)),
+            (tt, (WAL, WAL, E0C, A.add)),
+            (tt, (b("NU"), b("tm", 0, 128), b("BH"), A.mult)),
+            (cp, (OD, q_i)),
+            (ts, (b("AL"), b("BH"), WAL, None, A.mult)),
+            (ts, (PGE, OD, 100000.0, PG16, A.mult, A.add)),
+            (ts, (PGO, OD, -100000.0, 100000.0 - 16.0, A.mult, A.add)),
+            (ts, (b("swh"), b("sw", 0, 16), 0.5, None, A.add)),
+            (tt, (PGO, PGO, PG16, A.add)),
+            (ts, (b("E1"), b("jm11"), PGE, None, A.is_equal)),
+            (ts, (b("O1"), b("jm11"), PGO, None, A.is_equal))]
+
+    def filler(n):
+        for f, a in fill[:n]:
+            f(*a)
+        del fill[:n]
 
     def spawn_constants():
         ts(q_i, b("pp_i"), 1, None, A.bitwise_and)
@@ -281,8 +286,8 @@ def rank_program(g, core, T, topo):
         cp(b("c9"), b("c9f"))
 
     def arrival_constants():
-        ts(b("ID32"), b("ID"), -32.0, None, A.mult)
-        ts(b("ID8"), b("ID"), -8.0, None, A.mult)
+        ts(b("ID32"), b("ID"), -65536.0, None, A.mult)
+        ts(b("ID8"), b("ID"), -16384.0, None, A.mult)
         ts(b("MX"), b("J", 0, 16), PI, None, A.is_equal)
         for lo, hi in ((0, 128), (128, 256), (256, 320)):
             ts(b("CM", lo, hi), b("JI", 0, hi - lo), PI, 0.5, A.is_ge, A.mult)
@@ -293,12 +298,15 @@ def rank_program(g, core, T, topo):
 
     def q4(k):
         return 512 * k, 512 * k + 512
+    filler(5)
     for k in range(4):
         if k == 0:
             ts(b("X1", *q4(0)), b("XI", *q4(0)), 255, None, A.bitwise_and)
         if k < 3:
             ts(b("X1", *q4(k + 1)), b("XI", *q4(k + 1)), 255, None, A.bitwise_and)
+        filler(1)
         ts(b("NZ", *q4(k)), b("X1", *q4(k)), 128.0, None, A.not_equal)
+        filler(2)
         mm(b("P%d" % k), b("BH"), b("NZ", *q4(k)))
         act(b("SG", *q4(k)), b("P%d" % k), F.Sign, bias=-0.5)
         if k == 0:
@@ -333,6 +341,7 @@ def rank_program(g, core, T, topo):
             for x in range(16):
                 mm(b("P4", c1, 128), b("ZS", 15 - x, 143 - x), b("SG", e1 + x, e1 + x + 16 * (127 - c1) + 1, 16), x == 0, x == 15)
             spawn_constants()
+            child_constants()
         ts(b("Lb"), b("P4", 0, 128), 0.0, None, A.is_gt)
         mm(b("P5", 0, 128), b("BH"), b("Lb"))
         mm(b("P4", 128, 256), b("NU"), b("Lb"))
@@ -378,8 +387,6 @@ def rank_program(g, core, T, topo):
         act(b("P4", 0, 256), b("C"), F.Sign)
         act(b("P5", 0, 256), b("T6"), F.Identity, bias=128.0)
         ts(b("Dh"), b("T6"), 1.0 / 256.0, -2048.0, A.mult, A.add)
-        if t == 0:
-            child_constants()
         cp(b("Lg", 0, 1024), ind(b("HM"), b("Du", 0, 64)))
         for h in range(2):
             mm(b("P3", 16 * h, 16 * h + 16), b("Dh", 128 * h, 128 * h + 128), b("WT"))
@@ -451,8 +458,7 @@ def rank_program(g, core, T, topo):
                 mm(b3("Q0", slice(0, 4), slice(par, par + 16)), b(nh, 6 - 2 * j, 134 - 2 * j), b3("CH", slice(j, None, 4), full), False, j == 3)
         cp(b("fou"), b("fo3"))
         tt(b("ow1"), CHW, vr, A.is_equal)
-        tt(b("xg"), b("xf"), b("P0", 256, 512), A.add)
-        mm(b("P0", 0, 256), b("PAR"), b("ow1"))
+        mm(b("P4", 0, 256), b("PAR"), b("ow1"))
         tt(b("FK"), b("Fl"), b("P2", 0, 256), A.mult)
         vtr(b3("R4"), b3("Q0", slice(0, 4), full))
         cp(b3("ci"), b3("R4", full, slice(0, 8)))
@@ -460,15 +466,16 @@ def rank_program(g, core, T, topo):
         ts(b3("ca"), b3("ci"), 4095, None, A.bitwise_and)
         tt(b("iv2"), b("iv"), b("dm8"), A.max)
         tt(b("ch"), b3("ca", full, slice(0, 8, 2)), b3("ca", full, slice(1, 8, 2)), A.mult)
-        tt(b("cc"), b("FK"), b("P0", 0, 256), A.mult)
+        tt(b("xg"), b("xf"), b("P0", 256, 512), A.add)
         ts(b("ow"), b("ch"), 5, 7, A.arith_shift_right, A.bitwise_and)
-        tt(b("PK"), b("cc"), CHW, A.add)
+        tt(b("cc"), b("FK"), b("P4", 0, 256), A.mult)
         tt(b("own"), b("ow"), b("iv2"), A.add)
         for o in range(9):
             ts(b("O", 16 * o, 16 * o + 16), b("own"), float(o), None, A.is_equal if o < 8 else A.is_ge)
         mm(b("P3", 0, 144), b("BH"), b("O"))
         mm(b("P5", 0, 144), b("NU"), b("O"), True, False)
         mm(b("P5", 0, 144), b("e0h"), b("c9"), False, True)
+        tt(b("PK"), b("cc"), CHW, A.add)
         scan(b("I9"), b("m16", 0, 144), b("P3", 0, 144), A.mult, A.add)
         tt(b("A9"), b("I9"), b("P5", 0, 144), A.add)
         tt(b("s9"), b("A9"), b("O"), A.mult)
@@ -502,12 +509,21 @@ def rank_program(g, core, T, topo):
         cp(b(LA, at, at + CAP), b(SL, 256 * me, 256 * me + CAP))
         if t == 0:
             arrival_constants()
+        else:
+            for k in range(4):
+                act(b("SG", *q4(k)), b("X", TR + 512 * k, TR + 512 * k + 512), F.Sign)
+                mm(b("P%d" % (1 + k)), b("AL"), b("SG", *q4(k)))
+            for k in range(4):
+                q = (TR + 512 * k, TR + 512 * k + 512)
+                tt(b("Y", *q), b("X", *q), b("P%d" % (1 + k)), A.subtract)
 
         def score(bank, lo):
             q = (lo, lo + 60)
             ts(b("k1", *q), b(bank, 0, 60), 0.0, None, A.is_equal)
             act(b("k2", *q), b(bank, 0, 60), F.Sign, bias=-THETA)
             mm(b("P4", *q), b("e0b"), b("kcm", *q), True, False)
+            k = lo // 60 - 1
+            mm(b("P4", *q), b("ID"), b3("ZH1", slice(4 * k, 4 * k + 4), slice(0, 15)) if lo else b3("ZH0", full, slice(0, 5)), False, False)
             mm(b("P4", *q), b("ID32"), b("k1", *q), False, False)
             mm(b("P4", *q), b("ID8"), b("k2", *q), False, True)
 
@@ -534,25 +550,33 @@ def rank_program(g, core, T, topo):
             wp, n, ways = w + 1, 16 * w, w // 5
             a0, z0 = 16 * c0, 960 * part
             A16 = b3("A16", slice(c0, c2), full)
-            ts(A16, b(LA, a0, a0 + n), M23, -M23, A.add, A.add)
-            for par, nh in ((0, "EH"), (16, "OH")):
-                for j in range(ways):
-                    mm(b3("Q1p", slice(0, 5), slice(par, par + 16)), b(nh, 6 - 2 * j, 134 - 2 * j),
-                       b3("A16", slice(c0 + j, c2, ways), full), j == 0, j == ways - 1)
-            ts(b("Q1", a0, a0 + n), A16, 256.0, 524288.0 + OFF - M31, A.mult, A.add)
-            vtr(b3("R5"), b3("Q1p", slice(0, 5), full))
-            cp(b3("ai5", full, slice(0, 2 * ways)), b3("R5", full, slice(0, 2 * ways)))
-            ts(b3("aa5", full, slice(0, 2 * ways)), b3("ai5", full, slice(0, 2 * ways)), 4095, None, A.bitwise_and)
-            u1, u2 = b3("aa5", full, slice(0, 2 * ways, 2)), b3("aa5", full, slice(1, 2 * ways, 2))
             s0 = 6 * part
             st = b("st", s0, s0 + wp)
-            ts(b("st", s0, s0 + w), u1, 2.0, 1.0, A.mult, A.add)
-            tt(b("ah", 0, w), u1, u2, A.mult)
-            act(b("s2", 0, wp), st, F.Copy, scale=2.0)
-            act(b("s2", wp, 2 * wp), st, F.Copy, scale=2.0)
-            act(b("s4", 0, 2 * wp), b("s2", 0, 2 * wp), F.Copy, scale=2.0)
-            act(b("s4", 2 * wp, 4 * wp), b("s2", 0, 2 * wp), F.Copy, scale=2.0)
-            act(b("s8", 0, 4 * wp), b("s4", 0, 4 * wp), F.Copy, scale=2.0)
+            u1, u2 = b3("aa5", full, slice(0, 2 * ways, 2)), b3("aa5", full, slice(1, 2 * ways, 2))
+            ai5, aa5, R5 = [b3(x, full, slice(0, 2 * ways)) for x in ("ai5", "aa5", "R5")]
+
+            def orbitals():
+                ts(A16, b(LA, a0, a0 + n), M23, -M23, A.add, A.add)
+                for par, nh in ((0, "EH"), (16, "OH")):
+                    for j in range(ways):
+                        mm(b3("Q1p", slice(0, 5), slice(par, par + 16)), b(nh, 6 - 2 * j, 134 - 2 * j),
+                           b3("A16", slice(c0 + j, c2, ways), full), j == 0, j == ways - 1)
+
+            def numbers():
+                ts(b("st", s0, s0 + w), u1, 2.0, 1.0, A.mult, A.add)
+                tt(b("ah", 0, w), u1, u2, A.mult)
+                act(b("s2", 0, wp), st, F.Copy, scale=2.0)
+                act(b("s2", wp, 2 * wp), st, F.Copy, scale=2.0)
+                act(b("s4", 0, 2 * wp), b("s2", 0, 2 * wp), F.Copy, scale=2.0)
+                act(b("s4", 2 * wp, 4 * wp), b("s2", 0, 2 * wp), F.Copy, scale=2.0)
+                act(b("s8", 0, 4 * wp), b("s4", 0, 4 * wp), F.Copy, scale=2.0)
+
+            def first():
+                ts(b("Z", 0, w), b("ah", 0, w), 8, V - 1, A.arith_shift_right, A.bitwise_and)
+                cp(b("zu", 0, wp), b("Z", 0, wp))
+                tt(b("Z", wp, 2 * wp), b("Z", 0, wp), st, A.add)
+                if part:
+                    sums(0)
 
             def zm(lo, hi):
                 ts(b("Zm", lo * wp, hi * wp), b("Z", lo * wp, hi * wp), V - 1, None, A.bitwise_and)
@@ -560,19 +584,9 @@ def rank_program(g, core, T, topo):
             def zc(lo, hi):
                 cp(b("zu", lo * wp, hi * wp), b("Zm", lo * wp, hi * wp))
 
-            ts(b("Z", 0, w), b("ah", 0, w), 8, V - 1, A.arith_shift_right, A.bitwise_and)
-            ts(b("Hh", c0, c2), b("ah", 0, w), 8, V - 1, A.arith_shift_right, A.bitwise_and)
-            cp(b("zu", 0, wp), b("Z", 0, wp))
-            tt(b("Z", wp, 2 * wp), b("Z", 0, wp), st, A.add)
-            if part:
-                sums(0)
-            elif t == RO - 1:
-                for k in range(4):
-                    act(b("SG", *q4(k)), b("X", TR + 512 * k, TR + 512 * k + 512), F.Sign)
-                    mm(b("P%d" % (1 + k)), b("AL"), b("SG", *q4(k)))
-            for m in range(NP):
+            def probe(m):
                 if m == 1:
-                    zm(1, 2)
+                    zm(0, 2)
                     tt(b("Z", 2 * wp, 4 * wp), b("Z", 0, 2 * wp), b("s2", 0, 2 * wp), A.add)
                     zc(1, 2)
                     zm(2, 4)
@@ -584,6 +598,7 @@ def rank_program(g, core, T, topo):
                     zm(4, 12)
                 if m == 4:
                     zc(4, 12)
+                    cp(b3("ZH%d" % part), b("Zm", 0, 12 * wp))
                 if part and m > 2:
                     part0_tail(m - 3)
                 d = (z0 + n * m, z0 + n * m + n)
@@ -593,31 +608,38 @@ def rank_program(g, core, T, topo):
                     act(b("sq", *d), b("dd", *d), F.Square, bias=-M31 / 256.0, scale=1.0 / 256.0)
                 if part and m % 4 == 3:
                     k = m // 4 + 1
-                    sums(k)
                     if k > 1:
                         score("P%d" % (k - 1), 60 * (k - 1))
+                    sums(k)
                     if k == 2:
                         act(b("KS"), b("P4", 60, 120), F.Copy)
 
-        arrivals(0)
-        if t == RO - 1:
-            for k in range(4):
-                q = (TR + 512 * k, TR + 512 * k + 512)
-                tt(b("Y", *q), b("X", *q), b("P%d" % (1 + k)), A.subtract)
-        arrivals(1)
+            pre = [orbitals, lambda: ts(b("Q1", a0, a0 + n), A16, 256.0, 524288.0 + OFF - M31, A.mult, A.add),
+                   lambda: vtr(b3("R5"), b3("Q1p", slice(0, 5), full)), lambda: cp(ai5, R5),
+                   lambda: ts(aa5, ai5, 4095, None, A.bitwise_and), numbers, first]
+            return pre, probe
+
+        pre0, probe0 = arrivals(0)
+        pre1, probe1 = arrivals(1)
+        for f in pre0:
+            f()
+        for m in range(NP):
+            probe0(m)
+            if m > 5:
+                pre1.pop(0)()
+        for f in pre1:
+            f()
+        for m in range(NP):
+            probe1(m)
         tt(b("ac"), b(LA), b3("A16"), A.subtract)
         act(b("cq"), b("ac"), F.Identity, bias=128.0, scale=256.0)
-        score("P3", 180)
         tt(b("K1"), b("KS"), b("P4", 120, 180), A.min)
+        score("P3", 180)
         tt(b("K2"), b("K1"), b("P4", 180, 240), A.min)
         tt(b("K3", 0, 30), b("K2", 0, 30), b("K2", 30, 60), A.min)
         tt(b("km", 5, 20), b("K3", 0, 15), b("K3", 15, 30), A.min)
-        ts(b("ma"), b("km"), 15, None, A.bitwise_and)
+        ts(b("pm"), b("km"), V - 1, None, A.bitwise_and)
         ts(b("iv3"), b("km"), 0.0, -4096.0, A.is_ge, A.mult)
-        tt(b("ms", 0, 5), b("ma", 0, 5), b("st", 0, 5), A.mult)
-        tt(b("ms", 5, 20), b("ma", 5, 20), b("st", 6, 21), A.mult)
-        tt(b("pz"), b("ms"), b("Hh"), A.add)
-        ts(b("pm"), b("pz"), V - 1, None, A.bitwise_and)
         cp(b("pu"), b("pm"))
         tt(b("pvh"), b("pm"), b("iv3"), A.add)
         tt(b("pv"), b("pm"), b("iv3"), A.add)
@@ -653,7 +675,7 @@ def rank_program(g, core, T, topo):
             for x, y in rs:
                 ts(b("EQ", at, at + 16 * (y - x)), b("Pr", 16 * x, 16 * y), b("pv", k, k + 1), None, A.is_equal)
                 at += 16 * (y - x)
-            if size > 9:
+            if size > (10 if t < RO - 1 else 9):
                 act(b("jnk", e0, at), b("EQ", e0, at), F.Copy, accum=b("lw", k, k + 1))
             else:
                 small.append((k, e0, at))

from concourse.bass import DstId, RemoteDMATransfer
from concourse.mybir import AluOpType as A, AxisListType, ActivationFunctionType as F

N, V, CAP, S, RO, STEP, NP = 8, 2048, 40, 256, 2, 950, 12
AR = N * CAP
TR = 320
M31 = 1.5 * 2.0 ** 31
M27 = 1.5 * 2.0 ** 27
M23 = 1.5 * 2.0 ** 23
OFF = 2.0 ** 22
SENT = -22528
THETA = 1.14e10

_DT = {"f": "float32", "b": "bfloat16", "h": "float16", "i": "int32", "u": "uint16"}
_SBUF = """
f X:2368 Y:2368 J:256 JI:128 JG:128 PD:128 jm6:144 jm15:144 jm11:144 tm:144 tm2:144 tm3:144 tm4:144 col:32 ones:128 sw:20 swh:16
f Jp:256 dtr:20 c9f:144 m16:256 MX:16 E:128 U:136 acc:16 cb:16 vw:16 dm8:16 fo:16 fo2:16 fo3:16 T6:256 Sx:256 C:256 Ks:256 hb:16
f rk:16 VK:512 R1:256 R2:256 m1:256 FK:256 cc:256 PK:256 iv:16 iv2:16 own:16 I9:144 A9:144 plS:20 swS:20 t1:20 t2:20 t3:20 iv3:20
f SL0:2304 SL1:2304 LA0:320 LA1:320 Cf:256 xf:256 xg:256 Q1:320 ac:320 st:24 s2:32 s4:64 s8:64 dd:3840 KS:60 K1:60 K2:60 K3:32
f pv:20 lw:20 w1:320 xm:320 cn:320 ck:320 cq:320 xn:320 xo:320 R4:4,32 R5:5,32
i XI:2048 X1:2048 pp_i:1 pq_i:1 ai:16 pl:16 hp:16 hq:16 vi:16 vv:16 Fl:256 ch:16 ow:16 ah:16 Z:192 Zm:192 km:20 pm:20
i hi:2,16 ha:2,16 ci:4,8 ca:4,8 ai5:5,8 aa5:5,8
h NZ:2048 BH:128 NU:128 SU:128 SD:128 ID:128 BI:128 PAR:128 PK1:128 PK2:128 WT:16 EH:144 OH:144 E1:144 O1:144 e0h:128 RX:2048 CM:320
h c9:144 s9:144 Lb:128 G:256 Dh:256 VB:512 mA:256 mB:256 ow1:256 O:144 pvh:20 Pr:320
h CH:16,16 eq:16,16 A16:20,16 ZH0:12,6 ZH1:12,16
b HM:4096 SG:2064 SR:2048 BB:128 AL:128 ZS:144 I592:8 e0b:128 kc:128 kcm:240 ID32:128 ID8:128 m16b:320 cmp:1040 jnk:3040 Lg:4096
b Mn:4096 fsq:256 fsg:256 sq:3840 k1:240 k2:240 EQ:3040 DG:320 DS:320 esq:320 esg:320
u cu:16 plu:16 fou:16 Du:256 slu:16 zu:256 pu:20 eou:20
"""
_ALL, SCRATCH, _AT = {}, {}, {}
for _line in _SBUF.split("\n"):
    _w = _line.split()
    for _e in _w[1:]:
        _n, _s = _e.split(":")
        _ALL[_n] = ("sbuf", [128] + [int(_k) for _k in _s.split(",")], _DT[_w[0]])
for _n in ("P0", "P1", "P2", "P3", "P4", "P5"):
    _ALL[_n] = ("psum", [128, 512], "float32")
for _n in ("Q0", "Q1p"):
    _ALL[_n] = ("psum", [128, 16, 32], "float32")
_wide = {}
for _n, (_w, _sh, _d) in _ALL.items():
    if _w == "sbuf" and len(_sh) == 2 and _sh[1] <= 144:
        _AT[_n] = ("pack_" + _d, _wide.get(_d, 0))
        _wide[_d] = _AT[_n][1] + -(-_sh[1] // 16) * 16
    else:
        SCRATCH[_n] = (_w, _sh, _d)
for _d, _c in _wide.items():
    SCRATCH["pack_" + _d] = ("sbuf", [128, _c], _d)
SEMAPHORES = ["sv", "ss", "sp", "sg", "loc", "ar0", "ar1", "an0", "an1"] + ["d%d" % k for k in range(7)]
_PSUM = ("P0", "P1", "P2", "P3", "P4", "P5", "Q0", "Q1p")


def routes(src, T, topo):
    r = T.rank_of(src)
    ring = [T.cores[(r + k) % N] for k in range(1, N)]
    near = [d for d in ring if topo.chip(d) == topo.chip(src)]
    far = [d for d in ring if topo.chip(d) != topo.chip(src)]
    eng = topo.engines(src, far[0])
    n = len(eng)
    out = [(0, d, eng[k * n // 4:(k + 1) * n // 4]) for k, d in enumerate(far[:4])]
    out += [(1, d, eng[k * n // 2:(k + 1) * n // 2]) for k, d in enumerate(far[4:])]
    return out + [(0, d, [e for e in topo.engines(src, d) if e not in eng][:4]) for d in near]


def landing(dst, T, topo):
    near = [c for c in T.cores if topo.chip(c) == topo.chip(dst)]
    return [T.rank_of(c) for c in near + [c for c in T.cores if c not in near]]


def rank_program(g, core, T, topo):
    me = T.rank_of(core)
    if me is None:
        return
    queue = {"v": g.vector, "s": g.scalar, "p": g.tensor, "g": g, "y": g.sync}
    semof = {"v": "sv", "s": "ss", "p": "sp", "g": "sg"}
    cnt, known, snap, acc = {}, {e: {} for e in queue}, {}, {}
    BIGC = 1000000

    def b(n, lo=0, hi=None, step=1):
        if hi is None:
            hi = _ALL[n][1][1]
        if n in _AT:
            w, at = _AT[n]
            return T[w][:, at + lo:at + hi:step], [(w, at + lo, at + hi)]
        return T[n][:, lo:hi:step], [(n, lo, hi)]

    full = slice(None)

    def b3(n, s1=full, s2=full):
        return T[n][:, s1, s2], [(n, 0, BIGC)]

    def ind(w, o):
        return w[0].indirect(o[0]), w[1] + o[1]

    def need(e, reads, writes):
        want = {}
        for kind, keys in ((0, reads), (1, writes)):
            for (n, lo, hi) in keys:
                ps = n in _PSUM
                for lo2, hi2, k2, sem, val, e2 in acc.get(n, []):
                    if not ps and not (lo < hi2 and lo2 < hi):
                        continue
                    if e == "p" and e2 == "p" or not (kind or k2 or ps and e != e2):
                        continue
                    want[sem] = max(want.get(sem, 0), val)
        kn = known[e]
        for s, v in sorted(want.items(), key=lambda x: (x[0] == semof.get(e), x[0])):
            if kn.get(s, 0) >= v:
                continue
            queue[e].wait_ge(T.sem[s], v)
            kn[s] = v
            for s2, v2 in snap.get((s, v), {}).items():
                kn[s2] = max(kn.get(s2, 0), v2)

    def note(e, reads, writes, sem, val):
        for kind, keys in ((0, reads), (1, writes)):
            for (n, lo, hi) in keys:
                if n in _PSUM:
                    lo, hi = 0, BIGC
                lst = acc.setdefault(n, [])
                lst[:] = [r for r in lst if not (kind and lo <= r[0] and r[1] <= hi)
                          and not (r[5] == e and r[2] == kind and r[3] == sem and r[0] == lo and r[1] == hi)]
                lst.append((lo, hi, kind, sem, val, e))

    def op(e, call, outs, ins):
        reads = [k for x in ins for k in x[1]]
        writes = [k for x in outs for k in x[1]]
        need(e, reads, writes)
        s = semof[e]
        cnt[s] = v = cnt.get(s, 0) + 1
        call().then_inc(T.sem[s], 1)
        snap[(s, v)] = dict(known[e])
        note(e, reads, writes, s, v)

    def dma(e, out, in_, sem):
        need(e, in_[1], out[1])
        queue[e].dma_start(out=out[0], in_=in_[0]).then_inc(T.sem[sem], 16)
        snap[(sem, 16)] = dict(known[e])
        note(e, in_[1], out[1], sem, 16)

    def sc(x):
        return x[0] if isinstance(x, tuple) else x

    def ts(out, in0, s1, s2, op0, op1=None):
        ins = [in0] + [x for x in (s1, s2) if isinstance(x, tuple)]
        if op1 is None:
            op("v", lambda: g.vector.tensor_scalar(out[0], in0[0], sc(s1), None, op0), [out], ins)
        else:
            op("v", lambda: g.vector.tensor_scalar(out[0], in0[0], sc(s1), sc(s2), op0, op1), [out], ins)

    def tt(out, in0, in1, o):
        op("v", lambda: g.vector.tensor_tensor(out[0], in0[0], in1[0], o), [out], [in0, in1])

    def cp(out, in_):
        op("v", lambda: g.vector.tensor_copy(out[0], in_[0]), [out], [in_])

    def scan(out, d0, d1, o0, o1):
        op("v", lambda: g.vector.tensor_tensor_scan(out[0], d0[0], d1[0], 0.0, o0, o1), [out], [d0, d1])

    def red(out, in_, o):
        op("v", lambda: g.vector.tensor_reduce(out[0], in_[0], AxisListType.X, o), [out], [in_])

    def vtr(out, in_):
        op("v", lambda: g.vector.transpose(out[0], in_[0]), [out], [in_])

    def act(out, in_, f, bias=0.0, scale=1.0, accum=None):
        ins = [in_] + [x for x in (bias, scale) if isinstance(x, tuple)]
        if accum is None:
            op("s", lambda: g.scalar.activation(out[0], in_[0], f, bias=sc(bias), scale=sc(scale)), [out], ins)
        else:
            op("s", lambda: g.scalar.activation(out[0], in_[0], f, bias=sc(bias), scale=sc(scale), accum_out=accum[0]), [out, accum], ins)

    def mm(out, l, r, start=True, stop=True):
        op("p", lambda: g.tensor.matmul(out[0], l[0], r[0], start, stop), [out], [l, r])

    def iota(n, pat, base, cm, lo=0, hi=None):
        out = b(n, lo, hi)
        if _ALL[n][2] == "int32":
            op("g", lambda: g.iota(out[0], pat, base, cm), [out], [])
        else:
            op("g", lambda: g.iota(out[0], pat, base, cm, allow_small_or_imprecise_dtypes=True), [out], [])

    def gsel(out, in_):
        op("g", lambda: g.affine_select(out[0], in_[0], [[0, 8], [1, 16]], A.is_gt, 0.0, 0, 0), [out], [in_])

    for k in range(4):
        dma("y", b("XI", 512 * k, 512 * k + 512), (T.det[:, 512 * k:512 * k + 512], []), "d%d" % k)
    dma("s", b("HM"), (T.ham[:], []), "d4")

    iota("pp_i", [[0, 1]], 0, 1)
    iota("JG", [[1, 8], [0, 16]], 0, 0)
    iota("jm15", [[1, 144]], -15, 0)
    iota("JI", [[0, 8], [1, 16]], 0, 0)
    iota("PD", [[1, 128]], 0, -1)
    iota("J", [[1, 256]], 0, 0)
    iota("jm11", [[1, 144]], -11, 0)
    iota("ones", [[0, 128]], 1, 0)
    for k in range(6):
        iota("cmp", [[0, 1]], 128, 0, 144 * k + 128, 144 * k + 129)
    iota("U", [[0, 8]], -1, 0, 128, 136)
    iota("Jp", [[16, 4], [64, 4], [1, 16]], 0, 0)
    iota("jm6", [[1, 144]], -6, 0)
    iota("c9f", [[256, 9], [0, 16]], -1025, 0)
    for h in (0, 128):
        gsel(b("m16", h, h + 128), b("ones"))
    iota("VK", [[0, 512]], 0, 0)
    for o in range(N):
        iota("SL0", [[0, CAP]], SENT, 0, 256 * o, 256 * o + CAP)
    iota("kcm", [[2048, 12], [0, 5]], -16384, 0, 0, 60)
    iota("kcm", [[2048, 12], [0, 15]], -16384, 0, 60, 240)
    iota("lw", [[0, 20]], 0, 0)
    iota("st", [[0, 24]], 0, 0)
    iota("Z", [[0, 192]], 0, 0)
    for o in range(N):
        iota("SL1", [[0, CAP]], SENT, 0, 256 * o, 256 * o + CAP)

    PI, PG16, PGE, PGO, IM, ACOL, BCOL, W1, W2, SIG, WAL, P0C, PGE1, PGO1, SIGK, SIGM, E0C, N15, OD, N0 = \
        [b("col", k, k + 1) for k in range(20)]
    q_i = b("pq_i")
    ts(q_i, b("pp_i"), 15, None, A.bitwise_and)
    ts(PI, q_i, 1.0, None, A.mult)
    ts(q_i, b("pp_i"), 4, None, A.arith_shift_right)
    ts(PG16, q_i, 16.0, None, A.mult)
    ts(OD, q_i, 1.0, None, A.mult)
    ts(b("BH"), b("JG"), OD, None, A.is_equal)
    fill = [(ts, (b("ZS"), b("jm15"), PG16, None, A.is_equal)),
            (ts, (E0C, PI, 0.0, OFF, A.is_equal, A.mult)),
            (ts, (WAL, PI, 1.0, -128.0, A.is_equal, A.mult)),
            (ts, (b("tm", 0, 128), b("PD"), 0.0, -1.0, A.is_lt, A.mult)),
            (ts, (b("sw"), b("J", 0, 20), 16.0, PI, A.mult, A.add)),
            (ts, (q_i, q_i, 1, None, A.bitwise_and)),
            (tt, (WAL, WAL, E0C, A.add)),
            (tt, (b("NU"), b("tm", 0, 128), b("BH"), A.mult)),
            (cp, (OD, q_i)),
            (ts, (b("AL"), b("BH"), WAL, None, A.mult)),
            (ts, (PGE, OD, 100000.0, PG16, A.mult, A.add)),
            (ts, (PGO, OD, -100000.0, 100000.0 - 16.0, A.mult, A.add)),
            (ts, (b("swh"), b("sw", 0, 16), 0.5, None, A.add)),
            (tt, (PGO, PGO, PG16, A.add)),
            (ts, (b("E1"), b("jm11"), PGE, None, A.is_equal)),
            (ts, (b("O1"), b("jm11"), PGO, None, A.is_equal))]

    def filler(n):
        for f, a in fill[:n]:
            f(*a)
        del fill[:n]

    def spawn_constants():
        ts(q_i, b("pp_i"), 1, None, A.bitwise_and)
        ts(W1, PI, 13.0, 5.0, A.mult, A.add)
        ts(W2, PI, -14.0, 255.0, A.mult, A.add)
        ts(P0C, b("pp_i"), 0.0, None, A.is_equal)
        ts(SIG, q_i, -2.0, 1.0, A.mult, A.add)
        ts(IM, PI, -7.5, None, A.add)
        ts(N0, PI, 0.0, None, A.is_gt)
        ts(N15, PI, 15.0, None, A.is_lt)
        ts(SIGK, SIG, 1.0 / 256.0, None, A.mult)
        ts(SIGM, SIG, -1.0 / 256.0, None, A.mult)
        ts(PGE1, PGE, 1.0, None, A.add)
        ts(PGO1, PGO, 1.0, None, A.add)
        ts(b("WT", 0, 8), b("BH", 0, 128, 16), W1, None, A.mult)
        ts(b("WT", 8, 16), b("BH", 0, 128, 16), W2, None, A.mult)
        ts(b("e0b"), b("J", 0, 128), 0.0, P0C, A.mult, A.add)
        ts(b("kc"), b("JI"), -1.0, 7.5, A.mult, A.add)
        ts(b("I592"), b("BH", 0, 128, 16), 592.0, None, A.mult)
        ts(ACOL, N15, -1.0, None, A.mult)
        ts(BCOL, N0, -1.0, None, A.add)
        ts(b("dtr"), b("sw"), -1.0, float(TR), A.mult, A.add)
        ts(b("ID"), b("PD"), 0.0, None, A.is_equal)
        ts(b("SU"), b("PD"), -1.0, N0, A.is_equal, A.mult)
        ts(b("SD"), b("PD"), 1.0, N15, A.is_equal, A.mult)
        ts(b("BI"), b("PD"), 0.0, 8192.0, A.is_equal, A.mult)

    def child_constants():
        ts(b("tm2"), b("jm6"), PGE, W1, A.is_equal, A.mult)
        ts(b("tm"), b("jm6"), PGE1, W2, A.is_equal, A.mult)
        ts(b("tm3"), b("jm6"), PGO, W1, A.is_equal, A.mult)
        ts(b("tm4"), b("jm6"), PGO1, W2, A.is_equal, A.mult)
        ts(b("PAR"), b("BH"), SIG, None, A.mult)
        tt(b("EH"), b("tm"), b("tm2"), A.add)
        tt(b("OH"), b("tm3"), b("tm4"), A.add)
        ts(b("PK1"), b("BH"), SIGK, None, A.mult)
        ts(b("PK2"), b("BH"), SIGM, None, A.mult)
        cp(b("BB"), b("BH"))
        cp(b("e0h"), b("e0b"))
        cp(b("c9"), b("c9f"))

    def arrival_constants():
        ts(b("ID32"), b("ID"), -65536.0, None, A.mult)
        ts(b("ID8"), b("ID"), -16384.0, None, A.mult)
        ts(b("MX"), b("J", 0, 16), PI, None, A.is_equal)
        for lo, hi in ((0, 128), (128, 256), (256, 320)):
            ts(b("CM", lo, hi), b("JI", 0, hi - lo), PI, 0.5, A.is_ge, A.mult)
            cp(b("m16b", lo, hi), b("m16", 0, hi - lo))
        ts(b("swS"), b("sw"), 1.0 / 65536.0, None, A.mult)
        for x in range(16):
            ts(b("RX", 128 * x, 128 * x + 128), b("BH"), b("MX", x, x + 1), None, A.mult)

    def q4(k):
        return 512 * k, 512 * k + 512
    filler(5)
    for k in range(4):
        if k == 0:
            ts(b("X1", *q4(0)), b("XI", *q4(0)), 255, None, A.bitwise_and)
        if k < 3:
            ts(b("X1", *q4(k + 1)), b("XI", *q4(k + 1)), 255, None, A.bitwise_and)
        filler(1)
        ts(b("NZ", *q4(k)), b("X1", *q4(k)), 128.0, None, A.not_equal)
        filler(2)
        mm(b("P%d" % k), b("BH"), b("NZ", *q4(k)))
        act(b("SG", *q4(k)), b("P%d" % k), F.Sign, bias=-0.5)
        if k == 0:
            act(b("SG", V, V + 16), b("P0", 0, 16), F.Sign, bias=-0.5)

    XW = b("X", TR, TR + V)
    plan = {d: routes(d, T, topo) for d in T.cores}
    land = {d: landing(d, T, topo) for d in T.cores}
    near = sum(topo.chip(d) == topo.chip(core) for d in T.cores)
    own0 = min(land[core][:near])
    PART = ((0, near * CAP // 16), (near * CAP // 16, AR // 16))
    sent = [0]
    EQW, CHW = b3("eq"), b3("CH")

    for t in range(RO):
        start = STEP * (t + 1)
        if t:
            for k, (lo, hi) in enumerate(((0, V - start), (512, 1024), (V - start, 512), (1536, V), (1024, 1536))):
                x = b("X", TR + (lo + start) % V, TR + (hi - 1 + start) % V + 1)
                if k % 2:
                    act(b("SR", lo, hi), x, F.Sign)
                else:
                    ts(b("SR", lo, hi), x, 0.0, None, A.is_gt)
            for h in (0, 64):
                for x in range(16):
                    mm(b("P4", h, h + 64), b("ZS", 15 - x, 143 - x), b("SR", 16 * h + x, 16 * h + 1024, 16), x == 0, x == 15)
        else:
            c1 = (V - start + 15) // 16
            e1 = start + 16 * c1 - V
            for x in range(16):
                mm(b("P4", 0, c1), b("ZS", 15 - x, 143 - x), b("SG", start + x, start + x + 16 * (c1 - 1) + 1, 16), x == 0, x == 15)
            for x in range(16):
                mm(b("P4", c1, 128), b("ZS", 15 - x, 143 - x), b("SG", e1 + x, e1 + x + 16 * (127 - c1) + 1, 16), x == 0, x == 15)
            spawn_constants()
            child_constants()
        ts(b("Lb"), b("P4", 0, 128), 0.0, None, A.is_gt)
        mm(b("P5", 0, 128), b("BH"), b("Lb"))
        mm(b("P4", 128, 256), b("NU"), b("Lb"))
        if t == 0:
            for k in range(4):
                mm(b("P%d" % k), b("AL"), b("SG", *q4(k)))
        scan(b("E"), b("ones"), b("P5", 0, 128), A.mult, A.add)
        NA = 10
        for k in range(NA):
            act(b("jnk", 128 * k, 128 * k + 128), b("E"), F.Sign, bias=b("swh", k, k + 1), scale=-1.0, accum=b("acc", k, k + 1))
        tt(b("U", 0, 128), b("E"), b("P4", 128, 256), A.add)
        for k in range(NA, 17):
            o = 144 * (k - NA)
            if k < 16:
                ts(b("cmp", o, o + 128), b("E"), b("sw", k, k + 1), -2.0, A.is_gt, A.mult)
            if k > NA:
                red(b("acc", k - 1, k), b("cmp", o - 144, o - 15), A.add)
        ts(b("vw"), b("sw", 0, 16), b("E", 127, 128), None, A.is_lt)
        for j in range(4):
            ts(b("cu", 4 * j, 4 * j + 4), b("acc", j, 16, 4), 0.5, 64.0, A.mult, A.add)
        tt(b("G"), ind(b("U"), b("cu")), b("Jp"), A.is_le)
        ts(b("cb"), b("acc"), 8.0, 1024.0 + start, A.mult, A.add)
        ts(b("dm8"), b("vw"), -8.0, 8.0, A.mult, A.add)
        for par, n in ((0, "E1"), (16, "O1")):
            for j in range(4):
                mm(b3("Q0", slice(0, 4), slice(par, par + 16)), b(n, 11 - j, 139 - j), b("G", 64 * j, 64 * j + 64), j == 0, j == 3)
        if t == 0:
            for k in range(4):
                tt(b("X", TR + 512 * k, TR + 512 * k + 512), b("XI", *q4(k)), b("P%d" % k), A.add)
        vtr(b3("R4"), b3("Q0", slice(0, 4), full))
        tt(b("ai"), b("cb"), b3("R4", full, slice(0, 4)), A.add)
        ts(b("pl"), b("ai"), V - 1, None, A.bitwise_and)
        cp(b("plu"), b("pl"))
        act(b("Sx"), ind(XW, b("plu")), F.Identity, bias=-OFF)
        ts(b("T6"), ind(XW, b("plu")), M31, -(M31 + OFF), A.add, A.add)
        ts(b("Du"), b("T6"), 1.0 / 256.0, 4095.0, A.mult, A.min)
        tt(b("C"), b("Sx"), b("T6"), A.subtract)
        for lo, hi in ((64, 96), (0, 0), (96, 128), (128, 192), (192, 256)):
            if lo == hi:
                act(b("P0", 0, 256), b("C"), F.Abs)
            else:
                act(b("Lg", 16 * lo, 16 * hi), ind(b("HM"), b("Du", lo, hi)), F.Copy)
        act(b("P4", 0, 256), b("C"), F.Sign)
        act(b("P5", 0, 256), b("T6"), F.Identity, bias=128.0)
        ts(b("Dh"), b("T6"), 1.0 / 256.0, -2048.0, A.mult, A.add)
        cp(b("Lg", 0, 1024), ind(b("HM"), b("Du", 0, 64)))
        for h in range(2):
            mm(b("P3", 16 * h, 16 * h + 16), b("Dh", 128 * h, 128 * h + 128), b("WT"))
        for h in range(2):
            mm(b("P%d" % (1 + h), 0, 128), b("e0b"), b("kc"), True, False)

        def hash_step(k):
            if k == 0:
                cp(b3("hi"), b("P3", 0, 32))
            elif k == 1:
                ts(b3("ha"), b3("hi"), 4095, None, A.bitwise_and)
            elif k == 2:
                tt(b("hp"), b3("ha", full, slice(0, 8)), b3("ha", full, slice(8, 16)), A.mult)
            elif k == 3:
                ts(b("hq"), b("hp"), 5, None, A.arith_shift_right)
            elif k == 4:
                ts(b("hb"), b("hq"), 16.0, M27 + 16.0 * t, A.mult, A.add)
            else:
                ts(b("Fl"), b("C"), 0.25, -0.375, A.mult, A.add)

        for qd in range(4):
            lo, h = 64 * qd, qd // 2
            for k in range(16):
                tt(b("Mn", 256 * k + lo, 256 * k + lo + 64), b("Lg", 16 * lo + k, 16 * lo + 1024, 16), b("P0", lo, lo + 64), A.min)
                if qd == 1 and k % 2 == 0 and k < 12:
                    hash_step(k // 2)
                if qd % 2:
                    mm(b("P%d" % (1 + h), k, 128, 16), b("Mn", 256 * k + 128 * h, 256 * k + 128 * h + 128), b("I592"), False, k == 15)
            if qd == 2:
                scan(b("Ks", 0, 128), b("m16", 0, 128), b("P1", 0, 128), A.mult, A.max)
        tt(b("Cf"), b("C"), b("P4", 0, 256), A.subtract)
        act(b("fsq"), b("Cf"), F.Square)
        tt(b("xf"), b("Cf"), b("P5", 0, 256), A.add)
        mm(b("P0", 0, 256), b("BB"), b("fsq"))
        act(b("fsg"), b("P0", 0, 256), F.Sign, bias=-0.5)
        scan(b("Ks", 128, 256), b("m16", 0, 128), b("P2", 0, 128), A.mult, A.max)
        kmx = b("Ks", 15, 256, 16)
        tt(b("vi"), kmx, b("hb"), A.add)
        ts(b("rk"), kmx, M27, -M27, A.add, A.add)
        ts(b("vv"), b("vi"), 4, 4095, A.arith_shift_right, A.bitwise_and)
        tt(b("VK", 256, 512, 16), b("rk"), kmx, A.subtract)
        ts(b("VK", 0, 256, 16), b("vv"), -2048.0, None, A.add)
        scan(b("VB", 256, 512), b("m16"), b("VK", 256, 512), A.mult, A.add)
        scan(b("VB", 0, 256), b("m16"), b("VK", 0, 256), A.mult, A.add)
        tt(b("fo"), b("pl"), b("dtr", 0, 16), A.add)
        mm(b("P5", 0, 256), b("SU"), b("Dh"), True, False)
        mm(b("P1", 0, 256), b("SD"), b("Dh"), True, False)
        for x in (2, 3, 0, 1):
            mm(b("P4" if x > 1 else "P3", 128 * (x % 2), 128 * (x % 2) + 128), b("VB", 128 * x, 128 * x + 128), b("ID"))
        kr, vr = b("P4", 0, 256), b("P3", 0, 256)
        ts(b("mA"), kr, IM, ACOL, A.is_le, A.add)
        ts(b("mB"), kr, IM, BCOL, A.is_lt, A.add)
        mm(b("P5", 0, 256), b("BI"), b("mA"), False, True)
        mm(b("P1", 0, 256), b("BI"), b("mB"), False, True)
        mm(b("P2", 0, 256), b("PK1"), b("mA"), True, False)
        mm(b("P2", 0, 256), b("PK2"), b("mB"), False, True)
        mm(b("P0", 256, 512), b("AL"), b("fsg"))
        tt(b("fo2"), b("fo"), b("vw"), A.mult)
        tt(b("R1"), b("Dh"), b("P5", 0, 256), A.max)
        tt(b("R2"), b("Dh"), b("P1", 0, 256), A.min)
        tt(b("m1"), b("R1"), vr, A.min)
        tt(EQW, b("Dh"), vr, A.is_equal)
        tt(b("fo3"), b("fo2"), b("sw", 0, 16), A.add)
        tt(CHW, b("R2"), b("m1"), A.max)
        for par, ns, nh in ((0, "E1", "EH"), (16, "O1", "OH")):
            for j in range(4):
                mm(b3("Q0", slice(0, 4), slice(par, par + 16)), b(ns, 3 - j, 131 - j), b3("eq", slice(j, None, 4), full), j == 0, False)
            for j in range(4):
                mm(b3("Q0", slice(0, 4), slice(par, par + 16)), b(nh, 6 - 2 * j, 134 - 2 * j), b3("CH", slice(j, None, 4), full), False, j == 3)
        cp(b("fou"), b("fo3"))
        tt(b("ow1"), CHW, vr, A.is_equal)
        mm(b("P4", 0, 256), b("PAR"), b("ow1"))
        tt(b("FK"), b("Fl"), b("P2", 0, 256), A.mult)
        vtr(b3("R4"), b3("Q0", slice(0, 4), full))
        cp(b3("ci"), b3("R4", full, slice(0, 8)))
        ts(b("iv"), b3("R4", full, slice(8, 12)), 0.0, 8.0, A.is_gt, A.mult)
        ts(b3("ca"), b3("ci"), 4095, None, A.bitwise_and)
        tt(b("iv2"), b("iv"), b("dm8"), A.max)
        tt(b("ch"), b3("ca", full, slice(0, 8, 2)), b3("ca", full, slice(1, 8, 2)), A.mult)
        tt(b("xg"), b("xf"), b("P0", 256, 512), A.add)
        ts(b("ow"), b("ch"), 5, 7, A.arith_shift_right, A.bitwise_and)
        tt(b("cc"), b("FK"), b("P4", 0, 256), A.mult)
        tt(b("own"), b("ow"), b("iv2"), A.add)
        for o in range(9):
            ts(b("O", 16 * o, 16 * o + 16), b("own"), float(o), None, A.is_equal if o < 8 else A.is_ge)
        mm(b("P3", 0, 144), b("BH"), b("O"))
        mm(b("P5", 0, 144), b("NU"), b("O"), True, False)
        mm(b("P5", 0, 144), b("e0h"), b("c9"), False, True)
        tt(b("PK"), b("cc"), CHW, A.add)
        scan(b("I9"), b("m16", 0, 144), b("P3", 0, 144), A.mult, A.add)
        tt(b("A9"), b("I9"), b("P5", 0, 144), A.add)
        tt(b("s9"), b("A9"), b("O"), A.mult)
        for o in range(9):
            mm(b("P2", 0, 16), b("ID"), b("s9", 16 * o, 16 * o + 16), o == 0, o == 8)
        cp(ind(b("X"), b("fou")), b("xg"))
        ts(b("slu"), b("P2", 0, 16), 1024.0, None, A.add)
        SL, LA = "SL%d" % t, "LA%d" % t
        cp(ind(b(SL), b("slu")), b("PK"))
        for call in (0, 1):
            tr = []
            for cl, d, eng in plan[core]:
                if cl != call:
                    continue
                o, at = T.rank_of(d), CAP * land[d].index(me)
                need("g", b(SL, 256 * o, 256 * o + CAP)[1], [])
                tr.append(RemoteDMATransfer(
                    dst_ids=[DstId(rid=topo.addr(d)[0], pnc=topo.addr(d)[1])], dma_engine_mask=sum(1 << e for e in eng),
                    remote_sem=T.sem[("an%d" if topo.chip(d) == topo.chip(core) else "ar%d") % t],
                    src=T[SL][:, 256 * o:256 * o + CAP], dst=T[LA][:, at:at + CAP]))
                sent[0] += len(eng)
            g.remote_dma_fused(tr, local_sem=T.sem.loc)
        for d in T.cores:
            if d != core:
                nr = topo.chip(d) == topo.chip(core)
                tot = sum(len(e) for s in T.cores if s != core and (topo.chip(s) == topo.chip(core)) == nr
                          for _, x, e in plan[s] if x == core)
                at = CAP * land[core].index(T.rank_of(d))
                acc.setdefault(LA, []).append((at, at + CAP, 1, ("an%d" if nr else "ar%d") % t, tot, "r"))
        at = CAP * land[core].index(me)
        cp(b(LA, at, at + CAP), b(SL, 256 * me, 256 * me + CAP))
        if t == 0:
            arrival_constants()
        else:
            for k in range(4):
                act(b("SG", *q4(k)), b("X", TR + 512 * k, TR + 512 * k + 512), F.Sign)
                mm(b("P%d" % (1 + k)), b("AL"), b("SG", *q4(k)))
            for k in range(4):
                q = (TR + 512 * k, TR + 512 * k + 512)
                tt(b("Y", *q), b("X", *q), b("P%d" % (1 + k)), A.subtract)

        def score(bank, lo):
            q = (lo, lo + 60)
            ts(b("k1", *q), b(bank, 0, 60), 0.0, None, A.is_equal)
            act(b("k2", *q), b(bank, 0, 60), F.Sign, bias=-THETA)
            mm(b("P4", *q), b("e0b"), b("kcm", *q), True, False)
            k = lo // 60 - 1
            mm(b("P4", *q), b("ID"), b3("ZH1", slice(4 * k, 4 * k + 4), slice(0, 15)) if lo else b3("ZH0", full, slice(0, 5)), False, False)
            mm(b("P4", *q), b("ID32"), b("k1", *q), False, False)
            mm(b("P4", *q), b("ID8"), b("k2", *q), False, True)

        def sums(k):
            for x in range(16):
                mm(b("P%d" % k, 0, 60), b("ZS", 15 - x, 143 - x), b("sq", 960 * k + x, 960 * k + 960, 16), x == 0, x == 15)

        def part0_tail(k):
            if k == 0:
                score("P0", 0)
                act(b("K3", 0, 30), b("P4", 0, 30), F.Copy)
            elif k == 2:
                tt(b("K2", 0, 30), b("K3", 0, 30), b("P4", 30, 60), A.min)
            elif k == 3:
                tt(b("K1", 0, 15), b("K2", 0, 15), b("K2", 15, 30), A.min)
            elif k == 4:
                tt(b("K2", 30, 35), b("K1", 0, 5), b("K1", 5, 10), A.min)
            elif k == 5:
                tt(b("km", 0, 5), b("K2", 30, 35), b("K1", 10, 15), A.min)

        def arrivals(part):
            c0, c2 = PART[part]
            w = c2 - c0
            wp, n, ways = w + 1, 16 * w, w // 5
            a0, z0 = 16 * c0, 960 * part
            A16 = b3("A16", slice(c0, c2), full)
            s0 = 6 * part
            st = b("st", s0, s0 + wp)
            u1, u2 = b3("aa5", full, slice(0, 2 * ways, 2)), b3("aa5", full, slice(1, 2 * ways, 2))
            ai5, aa5, R5 = [b3(x, full, slice(0, 2 * ways)) for x in ("ai5", "aa5", "R5")]

            def orbitals():
                ts(A16, b(LA, a0, a0 + n), M23, -M23, A.add, A.add)
                for par, nh in ((0, "EH"), (16, "OH")):
                    for j in range(ways):
                        mm(b3("Q1p", slice(0, 5), slice(par, par + 16)), b(nh, 6 - 2 * j, 134 - 2 * j),
                           b3("A16", slice(c0 + j, c2, ways), full), j == 0, j == ways - 1)

            def numbers():
                ts(b("st", s0, s0 + w), u1, 2.0, 1.0, A.mult, A.add)
                tt(b("ah", 0, w), u1, u2, A.mult)
                act(b("s2", 0, wp), st, F.Copy, scale=2.0)
                act(b("s2", wp, 2 * wp), st, F.Copy, scale=2.0)
                act(b("s4", 0, 2 * wp), b("s2", 0, 2 * wp), F.Copy, scale=2.0)
                act(b("s4", 2 * wp, 4 * wp), b("s2", 0, 2 * wp), F.Copy, scale=2.0)
                act(b("s8", 0, 4 * wp), b("s4", 0, 4 * wp), F.Copy, scale=2.0)

            def first():
                ts(b("Z", 0, w), b("ah", 0, w), 8, V - 1, A.arith_shift_right, A.bitwise_and)
                cp(b("zu", 0, wp), b("Z", 0, wp))
                tt(b("Z", wp, 2 * wp), b("Z", 0, wp), st, A.add)
                if part:
                    sums(0)

            def zm(lo, hi):
                ts(b("Zm", lo * wp, hi * wp), b("Z", lo * wp, hi * wp), V - 1, None, A.bitwise_and)

            def zc(lo, hi):
                cp(b("zu", lo * wp, hi * wp), b("Zm", lo * wp, hi * wp))

            def probe(m):
                if m == 1:
                    zm(0, 2)
                    tt(b("Z", 2 * wp, 4 * wp), b("Z", 0, 2 * wp), b("s2", 0, 2 * wp), A.add)
                    zc(1, 2)
                    zm(2, 4)
                if m == 2:
                    tt(b("Z", 4 * wp, 8 * wp), b("Z", 0, 4 * wp), b("s4", 0, 4 * wp), A.add)
                    zc(2, 4)
                    tt(b("Z", 8 * wp, 12 * wp), b("Z", 0, 4 * wp), b("s8", 0, 4 * wp), A.add)
                if m == 3:
                    zm(4, 12)
                if m == 4:
                    zc(4, 12)
                    cp(b3("ZH%d" % part), b("Zm", 0, 12 * wp))
                if part and m > 2:
                    part0_tail(m - 3)
                d = (z0 + n * m, z0 + n * m + n)
                tt(b("dd", *d), ind(XW, b("zu", wp * m, wp * m + w)), b("Q1", a0, a0 + n), A.subtract)
                if part or m % 4 == 3:
                    d = d if part else (z0 + n * (m - 3), z0 + n * m + n)
                    act(b("sq", *d), b("dd", *d), F.Square, bias=-M31 / 256.0, scale=1.0 / 256.0)
                if part and m % 4 == 3:
                    k = m // 4 + 1
                    if k > 1:
                        score("P%d" % (k - 1), 60 * (k - 1))
                    sums(k)
                    if k == 2:
                        act(b("KS"), b("P4", 60, 120), F.Copy)

            pre = [orbitals, lambda: ts(b("Q1", a0, a0 + n), A16, 256.0, 524288.0 + OFF - M31, A.mult, A.add),
                   lambda: vtr(b3("R5"), b3("Q1p", slice(0, 5), full)), lambda: cp(ai5, R5),
                   lambda: ts(aa5, ai5, 4095, None, A.bitwise_and), numbers, first]
            return pre, probe

        pre0, probe0 = arrivals(0)
        pre1, probe1 = arrivals(1)
        for f in pre0:
            f()
        for m in range(NP):
            probe0(m)
            if m > 5:
                pre1.pop(0)()
        for f in pre1:
            f()
        for m in range(NP):
            probe1(m)
        tt(b("ac"), b(LA), b3("A16"), A.subtract)
        act(b("cq"), b("ac"), F.Identity, bias=128.0, scale=256.0)
        tt(b("K1"), b("KS"), b("P4", 120, 180), A.min)
        score("P3", 180)
        tt(b("K2"), b("K1"), b("P4", 180, 240), A.min)
        tt(b("K3", 0, 30), b("K2", 0, 30), b("K2", 30, 60), A.min)
        tt(b("km", 5, 20), b("K3", 0, 15), b("K3", 15, 30), A.min)
        ts(b("pm"), b("km"), V - 1, None, A.bitwise_and)
        ts(b("iv3"), b("km"), 0.0, -4096.0, A.is_ge, A.mult)
        cp(b("pu"), b("pm"))
        tt(b("pvh"), b("pm"), b("iv3"), A.add)
        tt(b("pv"), b("pm"), b("iv3"), A.add)
        for x in range(16):
            mm(b("P5", x, AR, 16), b("RX", 128 * x, 128 * x + 128), b("pvh"))
        mm(b("P0", 0, AR), b("ID"), b("CM"), True, False)
        for x in range(16):
            mm(b("P0", x, AR, 16), b("ID"), b("pvh"), False, x == 15)
        act(b("xm"), ind(XW, b("pu")), F.Identity, bias=M31)
        act(b("P1", 0, AR), b("xm"), F.Identity, bias=-M31)
        tt(b("w1"), ind(XW, b("pu")), b("cq"), A.add)
        act(b("P2", 0, AR), b("Q1"), F.Identity, bias=M31 - OFF)
        ts(b("plS"), b("pv"), float(TR), 1.0 / 65536.0, A.add, A.mult)
        tt(b("cn"), b("w1"), b("P1", 0, AR), A.subtract)
        cp(b("Pr"), b("P5", 0, AR))
        ts(b("ck"), b("cn"), 255.0, 1.0, A.min, A.max)
        if t < RO - 1:
            act(b("esq"), b("ck"), F.Square, bias=-128.0)
            mm(b("P3", 0, AR), b("BB"), b("esq"))
            act(b("esg"), b("P3", 0, AR), F.Sign, bias=-0.5)
            mm(b("P4", 0, AR), b("AL"), b("esg"))
        o5 = own0 // near * PART[0][1]
        n5 = PART[0][1]
        rng = []
        for k in range(20):
            r = [(0, k), (n5, n5 + o5)] if k < n5 else [(n5 if k < n5 + o5 else 0, k)]
            rng.append((sum(y - x for x, y in r), k, [(x, y) for x, y in r if x < y]))
        at, small = 0, []
        for size, k, rs in sorted(rng, reverse=True):
            if not size:
                continue
            e0 = at
            for x, y in rs:
                ts(b("EQ", at, at + 16 * (y - x)), b("Pr", 16 * x, 16 * y), b("pv", k, k + 1), None, A.is_equal)
                at += 16 * (y - x)
            if size > (10 if t < RO - 1 else 9):
                act(b("jnk", e0, at), b("EQ", e0, at), F.Copy, accum=b("lw", k, k + 1))
            else:
                small.append((k, e0, at))
        tt(b("DG"), b("Pr"), b("P0", 0, AR), A.is_equal)
        for k, e0, e2 in small:
            red(b("lw", k, k + 1), b("EQ", e0, e2), A.add)
        scan(b("DS"), b("m16b"), b("DG"), A.mult, A.max)
        tt(b("xn"), b("ck"), b("P2", 0, AR), A.add)
        if t < RO - 1:
            tt(b("xo"), b("xn"), b("P4", 0, AR), A.add)
        tt(b("t1"), b("plS"), b("DS", 15, AR, 16), A.subtract)
        tt(b("t2"), b("t1"), b("lw"), A.subtract)
        tt(b("t3"), b("t2"), b("swS"), A.max)
        ts(b("eou"), b("t3"), 65536.0, None, A.mult)
        if t < RO - 1:
            cp(ind(b("X"), b("eou")), b("xo"))
        else:
            cp(ind(b("Y"), b("eou")), b("xn"))
    for k, e in ((0, "y"), (1, "s")):
        dma(e, (T.y[:, 1024 * k:1024 * k + 1024], []), b("Y", TR + 1024 * k, TR + 1024 * k + 1024), "d%d" % (5 + k))
    for s in ("sv", "ss", "sp", "sg"):
        g.wait_ge(T.sem[s], cnt[s])
    for k in range(7):
        g.wait_ge(T.sem["d%d" % k], 16)
    g.wait_ge(T.sem.loc, sent[0])
